import numpy as np
import ml_dtypes


def mxq(x, axis, fmt="e4m3"):
    dtype, down = {"e4m3": (ml_dtypes.float8_e4m3fn, 7), "e5m2": (ml_dtypes.float8_e5m2, 14)}[fmt]
    v = np.moveaxis(np.asarray(x, np.float32).astype(ml_dtypes.bfloat16).astype(np.float64), axis, -1)
    blocks = v.reshape(v.shape[:-1] + (-1, 32))
    amax = np.abs(blocks).max(-1, keepdims=True)
    byte = np.maximum(np.where(amax > 0, np.frexp(amax)[1] - 1 + 127, 0) - down, 1)
    scale = np.exp2(byte - 127.0)
    codes = (blocks / scale).astype(np.float32).astype(dtype).astype(np.float64)
    return np.moveaxis((codes * scale).reshape(v.shape), -1, axis)


WIDE = False


def mx_kscale(k):
    if not WIDE:
        return np.ones(k)
    levels = np.array([10, -10, 5, -5, 0])
    if k % 512:
        return np.exp2(np.random.permutation(np.resize(levels, k // 32))).repeat(32)
    a = np.empty((k // 512, 16))
    for p in range(k // 512):
        a[p, :8] = np.random.permutation(np.resize(levels, 8))
        for g in range(8):
            far = levels[np.abs(levels - a[p, g]) >= 10]
            a[p, g + 8] = far[np.random.randint(len(far))]
    return np.exp2(a.ravel()).repeat(32)


def f64(x):
    return np.asarray(x).astype(np.float64)


def striped(idx):
    return np.tile(np.asarray(idx).reshape(-1, 16).T, (8, 1)).astype(np.uint16)


def unstriped(offs):
    return offs[:16].T.reshape(-1).astype(np.int64)


E2M1 = np.array([0.0, 0.5, 1.0, 1.5, 2.0, 3.0, 4.0, 6.0, -0.0, -0.5, -1.0, -1.5, -2.0, -3.0, -4.0, -6.0])


def pack_weight(w, fmt):
    k, n = w.shape
    w = f64(np.asarray(w, np.float32).astype(ml_dtypes.bfloat16)).reshape(k // 32, 32, n)
    amax = np.abs(w).max(1)
    if fmt == "e4m3":
        byte = np.frexp(amax)[1] - 1 + 127 - 7
    else:
        mant, ex = np.frexp(amax / 6.0)
        byte = np.where(mant > 0.5, ex, ex - 1) + 127
    byte = np.clip(np.where(amax > 0, byte, 1), 1, 254)
    scaled = (w * np.exp2(127.0 - byte)[:, None, :]).reshape(k, n).astype(np.float32)
    by_word = np.ascontiguousarray(scaled.reshape(k // 512, 128, 4, n).transpose(0, 1, 3, 2))
    if fmt == "e4m3":
        words = by_word.astype(ml_dtypes.float8_e4m3fn).view(np.uint8)
    else:
        c = by_word.astype(ml_dtypes.float4_e2m1fn).view(np.uint8) & 0xF
        words = (c[..., 0::2] | (c[..., 1::2] << 4)).reshape(k // 512, 128, 2 * n)
    return np.ascontiguousarray(words), np.ascontiguousarray(byte.astype(np.uint8).reshape(k // 512, 16, n))


def unpack_weight(words, scales, fmt):
    g, _, n = scales.shape
    words = np.ascontiguousarray(words).reshape(g, 128, n, -1)
    if fmt == "e4m3":
        vals = words.view(ml_dtypes.float8_e4m3fn).astype(np.float64)
    else:
        nib = np.empty((g, 128, n, 4), np.uint8)
        nib[..., 0::2] = words & 0xF
        nib[..., 1::2] = words >> 4
        vals = E2M1[nib]
    vals = vals * np.repeat(np.exp2(scales.astype(np.float64) - 127.0), 8, axis=1)[..., None]
    return vals.transpose(0, 1, 3, 2).reshape(g * 512, n)


B, N, T, D, DV, NQ = 1, 1024, 4096, 1024, 256, 128
PAGE = 512


def setup_inputs():
    n = np.random.standard_normal
    pages = np.random.permutation(T // PAGE)[:B * N // PAGE]
    idx = (pages[:, None] * PAGE + np.arange(PAGE)[None, :]).reshape(-1)
    s = mx_kscale(D)[:, None]
    u = np.ones(T)
    u[idx] = mx_kscale(B * N)
    r = np.random.uniform(0.5, 2.0, T)
    k = n((D, T)) / s
    v = n((DV, T)) / (u * r)
    kp = pack_weight(k, "e2m1")
    vp = pack_weight(v.T, "e4m3")
    return {
        "qT": (n((B, D, NQ)) * s * (0.60 / np.sqrt(D))).astype(np.float32),
        "k_words": np.ascontiguousarray(kp[0].reshape(D // 1024, 2, 128, T, 2).transpose(0, 2, 3, 1, 4)).reshape(D // 1024, 128, T, 4),
        "k_scales": kp[1],
        "v_words": vp[0],
        "v_scales": vp[1],
        "vs": np.tile(u * r, (128, 1)).astype(np.float32),
        "offs": striped(idx),
        "voffs": striped((pages[:, None] * DV + np.arange(DV)[None, :]).reshape(-1)),
    }


def reference(qT, k_words, k_scales, v_words, v_scales, vs, offs, voffs):
    idx = unstriped(offs)
    k = unpack_weight(k_words.reshape(D // 1024, 128, T, 2, 2).transpose(0, 3, 1, 2, 4).reshape(D // 512, 128, 2 * T), k_scales, "e2m1")
    v = unpack_weight(v_words, v_scales, "e4m3")
    v = v.reshape(T // 512, 512, DV)[unstriped(voffs)[::DV] // DV].reshape(B, N, DV)
    pick = lambda x: x[:, idx].reshape(x.shape[0], B, N).transpose(1, 0, 2)
    q = f64(qT)
    score = mxq(q, 1, "e4m3").transpose(0, 2, 1) @ pick(k)
    m = score.max(-1, keepdims=True)
    p = np.exp(score - m)
    total = p.sum(-1, keepdims=True)
    w = p * pick(f64(vs))[:, :1, :]
    y = mxq(w, 2, "e4m3") @ v
    y = y / total
    return y

@@ -1,0 +1,168 @@
+from contextlib import ExitStack
+
+import concourse.mybir as mybir
+from concourse.masks import make_identity
+
+N, T, D, DV, NQ = 1024, 4096, 1024, 256, 128
+PAGE = 512
+P = 128
+PACK = 4
+PAGES = N // PAGE
+POOL_PAGES = T // PAGE
+PASSES = D // PAGE
+
+FLOPS = 2 * NQ * N * (D + DV)
+BYTES = 4 * D * NQ + 4 * P * T + PASSES * 16 * T + 4 * P * POOL_PAGES * DV + POOL_PAGES * 16 * DV + 4 * T + 2 * P * (N + PAGES * DV) // 16 + 4 * NQ * DV
+
+F32 = mybir.dt.float32
+BF16 = mybir.dt.bfloat16
+I32 = mybir.dt.int32
+U32 = mybir.dt.uint32
+U16 = mybir.dt.uint16
+U8 = mybir.dt.uint8
+FP8X4 = mybir.dt.float8_e4m3fn_x4
+FP4X4 = mybir.dt.float4_e2m1fn_x4
+ALU = mybir.AluOpType
+ACT = mybir.ActivationFunctionType
+SHIFT = 16
+EXP_COLS = 256
+
+
+def tile_attend_pkv4_soft_kernel(tc, qT, k_words, k_scales, v_words, v_scales, vs, offs, voffs, out):
+    nc = tc.nc
+    with ExitStack() as ctx:
+        lists = ctx.enter_context(tc.tile_pool(name="lists", bufs=1))
+        sb = ctx.enter_context(tc.tile_pool(name="sb", bufs=1))
+        ps = ctx.enter_context(tc.psum_pool(name="ps", bufs=1))
+
+        k_list = lists.tile([P, N // 16], U16, name="k_list")
+        v_list = lists.tile([P, PAGES * DV // 16], U16, name="v_list")
+
+        k_scale_pool = sb.tile([P, T], U8, name="k_scale_pool", tag="then_ident", align_bytes=64)
+        vs_pool = sb.tile([P, T], F32, name="vs_pool", align_bytes=64)
+        v_scale_pool = sb.tile([P, POOL_PAGES * DV], U8, name="v_scale_pool", align_bytes=64)
+        k_plane1 = sb.tile([P, N], U8, name="k_plane1", align_bytes=64)
+        k_pool = sb.tile([P, T], I32, name="k_pool", align_bytes=64)
+        v_pool = sb.tile([P, POOL_PAGES * DV], I32, name="v_pool", align_bytes=64)
+        q_raw = sb.tile([P, PASSES, PACK, NQ], F32, name="q_raw", align_bytes=64)
+
+        nc.vector.memset(k_scale_pool[:].bitcast(I32), 0)
+        nc.vector.memset(vs_pool[:], 0.0)
+        nc.vector.memset(v_scale_pool[:].bitcast(I32), 0)
+        nc.vector.memset(k_plane1[:].bitcast(I32), 0)
+
+        nc.sync.dma_start(k_list[:], offs)
+        nc.sync.dma_start(v_list[:], voffs)
+        k_scale_rows = k_scales.bitcast(I32).rearrange("o (a r) c -> r a o c", r=4)
+        for r in range(4):
+            nc.scalar.dma_start(k_scale_pool[:].bitcast(I32)[r:P:SHIFT, :], k_scale_rows[r])
+        nc.sync.dma_start(q_raw[:].rearrange("p o j w -> p o (j w)"),
+                          qT[0].rearrange("(o p j) w -> p o (j w)", o=PASSES, j=PACK))
+        nc.sync.dma_start(k_pool[:], k_words[0].rearrange("g t b -> g (t b)").bitcast(I32))
+        nc.scalar.dma_start(vs_pool[0:1, :], vs[0:1, :])
+        v_scale_rows = v_scales.bitcast(I32).rearrange("u (a r) c -> r a u c", r=4)
+        for r in range(4):
+            nc.gpsimd.dma_start(
+                v_scale_pool[:].bitcast(I32)[r:P:32, :].rearrange("p (u c) -> p u c", u=POOL_PAGES), v_scale_rows[r])
+        nc.sync.dma_start(v_pool[:].rearrange("g (u e) -> g u e", u=POOL_PAGES),
+                          v_words.rearrange("u g e r -> g u (e r)").bitcast(I32))
+
+        k_plane0 = sb.tile([P, N], U8, name="k_plane0", align_bytes=64)
+        nc.vector.tensor_copy(k_plane0[:], k_scale_pool[:].indirect(k_list[:]))
+        nc.scalar.dma_start(k_plane1[:].bitcast(I32)[0:P - SHIFT, :], k_plane0[:].bitcast(I32)[SHIFT:P, :])
+        ident = sb.tile([P, P], F32, name="ident", tag="then_ident", align_bytes=64)
+        make_identity(nc, ident[:])
+        k_planes = [k_plane0, k_plane1]
+
+        q_bf = sb.tile([P, PASSES, NQ, PACK], BF16, name="q_bf", align_bytes=64)
+        nc.scalar.copy(q_bf[:], q_raw[:].rearrange("p o j w -> p o w j"))
+
+        vs_row = sb.tile([P, N], F32, name="vs_row", align_bytes=64)
+        nc.vector.tensor_copy(vs_row[:], vs_pool[:].indirect(k_list[:]))
+        vs_cols = []
+        for g in range(PAGES):
+            turned = ps.tile([P, PACK, P], F32, name="vs_turned%d" % g)
+            for t in range(PACK):
+                nc.tensor.transpose(turned[:, t, :], vs_row[:, g * PAGE + t:(g + 1) * PAGE:PACK], ident[:])
+            cols = sb.tile([P, PACK], F32, name="vs_cols%d" % g)
+            nc.scalar.copy(cols[:], turned[:, :, 0])
+            vs_cols.append(cols)
+
+        q_codes = sb.tile([P, PASSES * NQ], U32, name="q_codes", align_bytes=64)
+        q_scale = sb.tile([P, PASSES * NQ], U8, name="q_scale", align_bytes=64)
+        nc.vector.quantize_mx(out=q_codes[:].bitcast(FP8X4), scales=q_scale[:],
+                              in_=q_bf[:].rearrange("p o w j -> p (o w j)"))
+
+        v_plane0 = sb.tile([P, DV], U8, name="v_plane0", align_bytes=64)
+        nc.vector.tensor_copy(v_plane0[:], v_scale_pool[:].indirect(v_list[:, 0:DV // 16]))
+
+        scores = []
+        for g in range(PAGES):
+            pairs = sb.tile([P, PAGE], U32, name="k_pairs%d" % g, tag="k_pairs%d" % g, align_bytes=64)
+            nc.vector.tensor_copy(pairs[:], k_pool[:].bitcast(U32).indirect(
+                k_list[:, g * PAGE // 16:(g + 1) * PAGE // 16]))
+            halves = pairs[:].bitcast(U16).rearrange("p (n o) -> p o n", o=PASSES)
+            score = ps.tile([P, PAGE], F32, name="score%d" % g)
+            for o in range(PASSES):
+                words = sb.tile([P, PAGE], U16, name="k_words%d_%d" % (g, o), align_bytes=64)
+                nc.vector.tensor_copy(words[:], halves[:, o, :])
+                nc.tensor.matmul_mx(
+                    out=score[:],
+                    lhsT=q_codes[:, o * NQ:(o + 1) * NQ].bitcast(FP8X4),
+                    lhsT_scale=q_scale[:, o * NQ:(o + 1) * NQ],
+                    rhs=words[:].bitcast(FP4X4),
+                    rhs_scale=k_planes[o][:, g * PAGE:(g + 1) * PAGE],
+                    start=(o == 0), stop=(o == PASSES - 1))
+            scores.append(score)
+
+        neg = sb.tile([P, PAGES, PACK, P], F32, name="neg_scores", align_bytes=64)
+        neg_max0 = sb.tile([P, 1], F32, name="neg_max0", tag="order", align_bytes=64)
+        neg_max = sb.tile([P, 1], F32, name="neg_max")
+        nc.vector.tensor_scalar(neg[:, 0], scores[0][:].rearrange("q (s t) -> q t s", t=PACK), -1.0, None,
+                                op0=ALU.mult, op1=ALU.min, accum_out=neg_max0[:])
+        v_plane1 = sb.tile([P, DV], U8, name="v_plane1", tag="k_pairs1", align_bytes=64)
+        nc.vector.tensor_copy(v_plane1[:], v_scale_pool[:].indirect(v_list[:, DV // 16:2 * DV // 16]))
+        v_planes = [v_plane0, v_plane1]
+        nc.vector.tensor_scalar(neg[:, 1], scores[1][:].rearrange("q (s t) -> q t s", t=PACK), -1.0, neg_max0[:],
+                                op0=ALU.mult, op1=ALU.min, accum_out=neg_max[:])
+
+        v_codes = sb.tile([P, PAGES * DV], U32, name="v_codes", tag="order", align_bytes=64)
+        nc.vector.tensor_copy(v_codes[:], v_pool[:].bitcast(U32).indirect(v_list[:]))
+
+        prob = sb.tile([P, N], F32, name="prob", align_bytes=64)
+        sums = sb.tile([P, N // EXP_COLS], F32, name="sums")
+        neg_flat = neg[:].rearrange("q g t s -> q (g t s)")
+        for c in range(N // EXP_COLS):
+            cs = slice(c * EXP_COLS, (c + 1) * EXP_COLS)
+            nc.scalar.activation(prob[:, cs], neg_flat[:, cs], ACT.Exp, bias=neg_max[:], scale=-1.0,
+                                 accum_out=sums[:, c:c + 1])
+
+        y = ps.tile([P, DV], F32, name="y")
+        w_bf = []
+        for g in range(PAGES):
+            turned = ps.tile([P, PACK, NQ], F32, name="p_turned%d" % g)
+            for t in range(PACK):
+                c0 = g * PAGE + t * P
+                nc.tensor.transpose(turned[:, t, :], prob[:, c0:c0 + P], ident[:])
+            w = sb.tile([P, NQ, PACK], BF16, name="w_bf%d" % g, align_bytes=64)
+            nc.vector.tensor_tensor(w[:], turned[:].rearrange("s t q -> s q t"),
+                                    vs_cols[g][:].unsqueeze(1).to_broadcast([P, NQ, PACK]), ALU.mult)
+            w_bf.append(w)
+        for g in range(PAGES):
+            w_codes = sb.tile([P, NQ], U32, name="w_codes%d" % g, align_bytes=64)
+            w_scale = sb.tile([P, NQ], U8, name="w_scale%d" % g, align_bytes=64)
+            nc.vector.quantize_mx(out=w_codes[:].bitcast(FP8X4), scales=w_scale[:],
+                                  in_=w_bf[g][:].rearrange("s q t -> s (q t)"))
+            nc.tensor.matmul_mx(
+                out=y[:], lhsT=w_codes[:].bitcast(FP8X4), lhsT_scale=w_scale[:],
+                rhs=v_codes[:, g * DV:(g + 1) * DV].bitcast(FP8X4),
+                rhs_scale=v_planes[g][:],
+                start=(g == 0), stop=(g == PAGES - 1))
+
+        total = sb.tile([P, 1], F32, name="total")
+        nc.vector.tensor_reduce(total[:], sums[:], mybir.AxisListType.X, ALU.add)
+        inv = sb.tile([P, 1], F32, name="inv")
+        nc.vector.reciprocal(inv[:], total[:])
+        res = sb.tile([P, DV], F32, name="res", align_bytes=64)
+        nc.vector.tensor_scalar(res[:], y[:], inv[:], None, op0=ALU.mult)
+        nc.sync.dma_start(out[0], res[:])

@@ -38,14 +38,16 @@ def tile_attend_pkv4_soft_kernel(tc, qT, k_words, k_scales, v_words, v_scales, v
         k_list = lists.tile([P, N // 16], U16, name="k_list")
         v_list = lists.tile([P, PAGES * DV // 16], U16, name="v_list")
 
-        k_scale_pool = sb.tile([P, T], U8, name="k_scale_pool", tag="then_ident", align_bytes=64)
-        vs_pool = sb.tile([P, T], F32, name="vs_pool", align_bytes=64)
+        k_scale_pool = sb.tile([P, T], U8, name="k_scale_pool", align_bytes=64)
+        vs_pool = sb.tile([P, T], F32, name="vs_pool", tag="k_pairs0", align_bytes=64)
         v_scale_pool = sb.tile([P, POOL_PAGES * DV], U8, name="v_scale_pool", align_bytes=64)
         k_plane1 = sb.tile([P, N], U8, name="k_plane1", align_bytes=64)
         k_pool = sb.tile([P, T], I32, name="k_pool", align_bytes=64)
         v_pool = sb.tile([P, POOL_PAGES * DV], I32, name="v_pool", align_bytes=64)
         q_raw = sb.tile([P, PASSES, PACK, NQ], F32, name="q_raw", align_bytes=64)
 
+        ident = sb.tile([P, P], F32, name="ident", align_bytes=64)
+        make_identity(nc, ident[:])
         nc.vector.memset(k_scale_pool[:].bitcast(I32), 0)
         nc.vector.memset(vs_pool[:], 0.0)
         nc.vector.memset(v_scale_pool[:].bitcast(I32), 0)
@@ -55,14 +57,14 @@ def tile_attend_pkv4_soft_kernel(tc, qT, k_words, k_scales, v_words, v_scales, v
         nc.sync.dma_start(v_list[:], voffs)
         k_scale_rows = k_scales.bitcast(I32).rearrange("o (a r) c -> r a o c", r=4)
         for r in range(4):
-            nc.scalar.dma_start(k_scale_pool[:].bitcast(I32)[r:P:SHIFT, :], k_scale_rows[r])
+            nc.sync.dma_start(k_scale_pool[:].bitcast(I32)[r:P:SHIFT, :], k_scale_rows[r])
         nc.sync.dma_start(q_raw[:].rearrange("p o j w -> p o (j w)"),
                           qT[0].rearrange("(o p j) w -> p o (j w)", o=PASSES, j=PACK))
         nc.sync.dma_start(k_pool[:], k_words[0].rearrange("g t b -> g (t b)").bitcast(I32))
         nc.scalar.dma_start(vs_pool[0:1, :], vs[0:1, :])
         v_scale_rows = v_scales.bitcast(I32).rearrange("u (a r) c -> r a u c", r=4)
         for r in range(4):
-            nc.gpsimd.dma_start(
+            nc.scalar.dma_start(
                 v_scale_pool[:].bitcast(I32)[r:P:32, :].rearrange("p (u c) -> p u c", u=POOL_PAGES), v_scale_rows[r])
         nc.sync.dma_start(v_pool[:].rearrange("g (u e) -> g u e", u=POOL_PAGES),
                           v_words.rearrange("u g e r -> g u (e r)").bitcast(I32))
@@ -70,8 +72,6 @@ def tile_attend_pkv4_soft_kernel(tc, qT, k_words, k_scales, v_words, v_scales, v
         k_plane0 = sb.tile([P, N], U8, name="k_plane0", align_bytes=64)
         nc.vector.tensor_copy(k_plane0[:], k_scale_pool[:].indirect(k_list[:]))
         nc.scalar.dma_start(k_plane1[:].bitcast(I32)[0:P - SHIFT, :], k_plane0[:].bitcast(I32)[SHIFT:P, :])
-        ident = sb.tile([P, P], F32, name="ident", tag="then_ident", align_bytes=64)
-        make_identity(nc, ident[:])
         k_planes = [k_plane0, k_plane1]
 
         q_bf = sb.tile([P, PASSES, NQ, PACK], BF16, name="q_bf", align_bytes=64)

@@ -38,18 +38,16 @@ def tile_attend_pkv4_soft_kernel(tc, qT, k_words, k_scales, v_words, v_scales, v
         k_list = lists.tile([P, N // 16], U16, name="k_list")
         v_list = lists.tile([P, PAGES * DV // 16], U16, name="v_list")
 
-        k_scale_pool = sb.tile([P, T], U8, name="k_scale_pool", align_bytes=64)
-        vs_pool = sb.tile([P, T], F32, name="vs_pool", tag="k_pairs0", align_bytes=64)
+        k_scale_pool = sb.tile([P, T], U8, name="k_scale_pool", tag="q_codes", align_bytes=64)
+        vs_pool = sb.tile([P, T], F32, name="vs_pool", align_bytes=64)
         v_scale_pool = sb.tile([P, POOL_PAGES * DV], U8, name="v_scale_pool", align_bytes=64)
         k_plane1 = sb.tile([P, N], U8, name="k_plane1", align_bytes=64)
         k_pool = sb.tile([P, T], I32, name="k_pool", align_bytes=64)
         v_pool = sb.tile([P, POOL_PAGES * DV], I32, name="v_pool", align_bytes=64)
-        q_raw = sb.tile([P, PASSES, PACK, NQ], F32, name="q_raw", align_bytes=64)
+        q_raw = sb.tile([P, PASSES, PACK, NQ], F32, name="q_raw", tag="ident", align_bytes=64)
 
-        ident = sb.tile([P, P], F32, name="ident", align_bytes=64)
-        make_identity(nc, ident[:])
         nc.vector.memset(k_scale_pool[:].bitcast(I32), 0)
-        nc.vector.memset(vs_pool[:], 0.0)
+        nc.vector.memset(vs_pool[:].bitcast(I32), 0)
         nc.vector.memset(v_scale_pool[:].bitcast(I32), 0)
         nc.vector.memset(k_plane1[:].bitcast(I32), 0)
 
@@ -76,33 +74,36 @@ def tile_attend_pkv4_soft_kernel(tc, qT, k_words, k_scales, v_words, v_scales, v
 
         q_bf = sb.tile([P, PASSES, NQ, PACK], BF16, name="q_bf", align_bytes=64)
         nc.scalar.copy(q_bf[:], q_raw[:].rearrange("p o j w -> p o w j"))
+        ident = sb.tile([P, P], F32, name="ident", tag="ident", align_bytes=64)
+        make_identity(nc, ident[:])
 
         vs_row = sb.tile([P, N], F32, name="vs_row", align_bytes=64)
         nc.vector.tensor_copy(vs_row[:], vs_pool[:].indirect(k_list[:]))
         vs_cols = []
         for g in range(PAGES):
-            turned = ps.tile([P, PACK, P], F32, name="vs_turned%d" % g)
+            turned = ps.tile([P, PACK, P], F32, name="vs_turned%d" % g, tag="bank%d" % g)
             for t in range(PACK):
                 nc.tensor.transpose(turned[:, t, :], vs_row[:, g * PAGE + t:(g + 1) * PAGE:PACK], ident[:])
             cols = sb.tile([P, PACK], F32, name="vs_cols%d" % g)
             nc.scalar.copy(cols[:], turned[:, :, 0])
             vs_cols.append(cols)
 
-        q_codes = sb.tile([P, PASSES * NQ], U32, name="q_codes", align_bytes=64)
+        q_codes = sb.tile([P, PASSES * NQ], U32, name="q_codes", tag="q_codes", align_bytes=64)
         q_scale = sb.tile([P, PASSES * NQ], U8, name="q_scale", align_bytes=64)
         nc.vector.quantize_mx(out=q_codes[:].bitcast(FP8X4), scales=q_scale[:],
                               in_=q_bf[:].rearrange("p o w j -> p (o w j)"))
 
-        v_plane0 = sb.tile([P, DV], U8, name="v_plane0", align_bytes=64)
-        nc.vector.tensor_copy(v_plane0[:], v_scale_pool[:].indirect(v_list[:, 0:DV // 16]))
 
         scores = []
+        k_pairs = []
         for g in range(PAGES):
-            pairs = sb.tile([P, PAGE], U32, name="k_pairs%d" % g, tag="k_pairs%d" % g, align_bytes=64)
+            pairs = sb.tile([P, PAGE], U32, name="k_pairs%d" % g, align_bytes=64)
             nc.vector.tensor_copy(pairs[:], k_pool[:].bitcast(U32).indirect(
                 k_list[:, g * PAGE // 16:(g + 1) * PAGE // 16]))
-            halves = pairs[:].bitcast(U16).rearrange("p (n o) -> p o n", o=PASSES)
-            score = ps.tile([P, PAGE], F32, name="score%d" % g)
+            k_pairs.append(pairs)
+        for g in range(PAGES):
+            halves = k_pairs[g][:].bitcast(U16).rearrange("p (n o) -> p o n", o=PASSES)
+            score = ps.tile([P, PAGE], F32, name="score%d" % g, tag="bank%d" % g)
             for o in range(PASSES):
                 words = sb.tile([P, PAGE], U16, name="k_words%d_%d" % (g, o), align_bytes=64)
                 nc.vector.tensor_copy(words[:], halves[:, o, :])
@@ -115,14 +116,14 @@ def tile_attend_pkv4_soft_kernel(tc, qT, k_words, k_scales, v_words, v_scales, v
                     start=(o == 0), stop=(o == PASSES - 1))
             scores.append(score)
 
+        v_plane = sb.tile([P, PAGES * DV], U8, name="v_plane", align_bytes=64)
+        nc.vector.tensor_copy(v_plane[:], v_scale_pool[:].indirect(v_list[:]))
+
         neg = sb.tile([P, PAGES, PACK, P], F32, name="neg_scores", align_bytes=64)
         neg_max0 = sb.tile([P, 1], F32, name="neg_max0", tag="order", align_bytes=64)
         neg_max = sb.tile([P, 1], F32, name="neg_max")
         nc.vector.tensor_scalar(neg[:, 0], scores[0][:].rearrange("q (s t) -> q t s", t=PACK), -1.0, None,
                                 op0=ALU.mult, op1=ALU.min, accum_out=neg_max0[:])
-        v_plane1 = sb.tile([P, DV], U8, name="v_plane1", tag="k_pairs1", align_bytes=64)
-        nc.vector.tensor_copy(v_plane1[:], v_scale_pool[:].indirect(v_list[:, DV // 16:2 * DV // 16]))
-        v_planes = [v_plane0, v_plane1]
         nc.vector.tensor_scalar(neg[:, 1], scores[1][:].rearrange("q (s t) -> q t s", t=PACK), -1.0, neg_max0[:],
                                 op0=ALU.mult, op1=ALU.min, accum_out=neg_max[:])
 
@@ -156,7 +157,7 @@ def tile_attend_pkv4_soft_kernel(tc, qT, k_words, k_scales, v_words, v_scales, v
             nc.tensor.matmul_mx(
                 out=y[:], lhsT=w_codes[:].bitcast(FP8X4), lhsT_scale=w_scale[:],
                 rhs=v_codes[:, g * DV:(g + 1) * DV].bitcast(FP8X4),
-                rhs_scale=v_planes[g][:],
+                rhs_scale=v_plane[:, g * DV:(g + 1) * DV],
                 start=(g == 0), stop=(g == PAGES - 1))
 
         total = sb.tile([P, 1], F32, name="total")

@@ -24,8 +24,8 @@ FP8X4 = mybir.dt.float8_e4m3fn_x4
 FP4X4 = mybir.dt.float4_e2m1fn_x4
 ALU = mybir.AluOpType
 ACT = mybir.ActivationFunctionType
-SHIFT = 16
 EXP_COLS = 256
+VS_AT = 4 * PASSES * PACK * NQ
 
 
 def tile_attend_pkv4_soft_kernel(tc, qT, k_words, k_scales, v_words, v_scales, vs, offs, voffs, out):
@@ -33,47 +33,54 @@ def tile_attend_pkv4_soft_kernel(tc, qT, k_words, k_scales, v_words, v_scales, v
     with ExitStack() as ctx:
         lists = ctx.enter_context(tc.tile_pool(name="lists", bufs=1))
         sb = ctx.enter_context(tc.tile_pool(name="sb", bufs=1))
+        shared = ctx.enter_context(tc.tile_pool(name="shared", bufs=1))
         ps = ctx.enter_context(tc.psum_pool(name="ps", bufs=1))
 
         k_list = lists.tile([P, N // 16], U16, name="k_list")
         v_list = lists.tile([P, PAGES * DV // 16], U16, name="v_list")
 
         k_scale_pool = sb.tile([P, T], U8, name="k_scale_pool", tag="q_codes", align_bytes=64)
-        vs_pool = sb.tile([P, T], F32, name="vs_pool", align_bytes=64)
-        v_scale_pool = sb.tile([P, POOL_PAGES * DV], U8, name="v_scale_pool", align_bytes=64)
-        k_plane1 = sb.tile([P, N], U8, name="k_plane1", align_bytes=64)
+        vs_pool = shared.tile([P, T], F32, name="vs_pool", align_bytes=64, offset=VS_AT)
         k_pool = sb.tile([P, T], I32, name="k_pool", align_bytes=64)
-        v_pool = sb.tile([P, POOL_PAGES * DV], I32, name="v_pool", align_bytes=64)
-        q_raw = sb.tile([P, PASSES, PACK, NQ], F32, name="q_raw", tag="ident", align_bytes=64)
+        v_pool = sb.tile([P, POOL_PAGES * DV], I32, name="v_pool", tag="w_bf0", align_bytes=64)
+        q_raw = shared.tile([P, PASSES, PACK, NQ], F32, name="q_raw", align_bytes=64, offset=0)
 
         nc.vector.memset(k_scale_pool[:].bitcast(I32), 0)
         nc.vector.memset(vs_pool[:].bitcast(I32), 0)
-        nc.vector.memset(v_scale_pool[:].bitcast(I32), 0)
-        nc.vector.memset(k_plane1[:].bitcast(I32), 0)
 
         nc.sync.dma_start(k_list[:], offs)
         nc.sync.dma_start(v_list[:], voffs)
-        k_scale_rows = k_scales.bitcast(I32).rearrange("o (a r) c -> r a o c", r=4)
-        for r in range(4):
-            nc.sync.dma_start(k_scale_pool[:].bitcast(I32)[r:P:SHIFT, :], k_scale_rows[r])
+        nc.sync.dma_start(k_scale_pool[:].bitcast(I32)[0:P:4, :], k_scales.bitcast(I32).rearrange("o f c -> (o f) c"))
         nc.sync.dma_start(q_raw[:].rearrange("p o j w -> p o (j w)"),
                           qT[0].rearrange("(o p j) w -> p o (j w)", o=PASSES, j=PACK))
         nc.sync.dma_start(k_pool[:], k_words[0].rearrange("g t b -> g (t b)").bitcast(I32))
         nc.scalar.dma_start(vs_pool[0:1, :], vs[0:1, :])
+
+        q_bf = sb.tile([P, PASSES, NQ, PACK], BF16, name="q_bf", tag="ident", align_bytes=64)
+        nc.scalar.copy(q_bf[:], q_raw[:].rearrange("p o j w -> p o w j"))
+
+        v_scale_pool = shared.tile([P, POOL_PAGES * DV], U8, name="v_scale_pool", align_bytes=64, offset=0)
+        k_planes = shared.tile([P, PASSES * N], U8, name="k_planes", align_bytes=64, offset=POOL_PAGES * DV)
+        nc.gpsimd.memset(v_scale_pool[:].bitcast(I32), 0)
+        nc.gpsimd.memset(k_planes[:].bitcast(I32), 0)
         v_scale_rows = v_scales.bitcast(I32).rearrange("u (a r) c -> r a u c", r=4)
         for r in range(4):
-            nc.scalar.dma_start(
+            nc.sync.dma_start(
                 v_scale_pool[:].bitcast(I32)[r:P:32, :].rearrange("p (u c) -> p u c", u=POOL_PAGES), v_scale_rows[r])
+
+        k_scale_rows = sb.tile([P, N], U8, name="k_scale_rows", align_bytes=64)
+        nc.vector.tensor_copy(k_scale_rows[:], k_scale_pool[:].indirect(k_list[:]))
+        for o in range(PASSES):
+            for r in range(4):
+                nc.sync.dma_start(k_planes[:].bitcast(I32)[r:P:32, o * N // 4:(o + 1) * N // 4],
+                                  k_scale_rows[:].bitcast(I32)[64 * o + 4 * r:64 * (o + 1):16, :])
         nc.sync.dma_start(v_pool[:].rearrange("g (u e) -> g u e", u=POOL_PAGES),
                           v_words.rearrange("u g e r -> g u (e r)").bitcast(I32))
 
-        k_plane0 = sb.tile([P, N], U8, name="k_plane0", align_bytes=64)
-        nc.vector.tensor_copy(k_plane0[:], k_scale_pool[:].indirect(k_list[:]))
-        nc.scalar.dma_start(k_plane1[:].bitcast(I32)[0:P - SHIFT, :], k_plane0[:].bitcast(I32)[SHIFT:P, :])
-        k_planes = [k_plane0, k_plane1]
-
-        q_bf = sb.tile([P, PASSES, NQ, PACK], BF16, name="q_bf", align_bytes=64)
-        nc.scalar.copy(q_bf[:], q_raw[:].rearrange("p o j w -> p o w j"))
+        q_codes = sb.tile([P, PASSES * NQ], U32, name="q_codes", tag="q_codes", align_bytes=64)
+        q_scale = sb.tile([P, PASSES * NQ], U8, name="q_scale", align_bytes=64)
+        nc.vector.quantize_mx(out=q_codes[:].bitcast(FP8X4), scales=q_scale[:],
+                              in_=q_bf[:].rearrange("p o w j -> p (o w j)"))
         ident = sb.tile([P, P], F32, name="ident", tag="ident", align_bytes=64)
         make_identity(nc, ident[:])
 
@@ -88,16 +95,11 @@ def tile_attend_pkv4_soft_kernel(tc, qT, k_words, k_scales, v_words, v_scales, v
             nc.scalar.copy(cols[:], turned[:, :, 0])
             vs_cols.append(cols)
 
-        q_codes = sb.tile([P, PASSES * NQ], U32, name="q_codes", tag="q_codes", align_bytes=64)
-        q_scale = sb.tile([P, PASSES * NQ], U8, name="q_scale", align_bytes=64)
-        nc.vector.quantize_mx(out=q_codes[:].bitcast(FP8X4), scales=q_scale[:],
-                              in_=q_bf[:].rearrange("p o w j -> p (o w j)"))
-
 
         scores = []
         k_pairs = []
         for g in range(PAGES):
-            pairs = sb.tile([P, PAGE], U32, name="k_pairs%d" % g, align_bytes=64)
+            pairs = shared.tile([P, PAGE], U32, name="k_pairs%d" % g, align_bytes=64, offset=VS_AT + 4 * PAGE * g)
             nc.vector.tensor_copy(pairs[:], k_pool[:].bitcast(U32).indirect(
                 k_list[:, g * PAGE // 16:(g + 1) * PAGE // 16]))
             k_pairs.append(pairs)
@@ -112,19 +114,20 @@ def tile_attend_pkv4_soft_kernel(tc, qT, k_words, k_scales, v_words, v_scales, v
                     lhsT=q_codes[:, o * NQ:(o + 1) * NQ].bitcast(FP8X4),
                     lhsT_scale=q_scale[:, o * NQ:(o + 1) * NQ],
                     rhs=words[:].bitcast(FP4X4),
-                    rhs_scale=k_planes[o][:, g * PAGE:(g + 1) * PAGE],
+                    rhs_scale=k_planes[:, o * N + g * PAGE:o * N + (g + 1) * PAGE],
                     start=(o == 0), stop=(o == PASSES - 1))
             scores.append(score)
 
-        v_plane = sb.tile([P, PAGES * DV], U8, name="v_plane", align_bytes=64)
+        v_plane = shared.tile([P, PAGES * DV], U8, name="v_plane", align_bytes=64, offset=VS_AT)
         nc.vector.tensor_copy(v_plane[:], v_scale_pool[:].indirect(v_list[:]))
 
-        neg = sb.tile([P, PAGES, PACK, P], F32, name="neg_scores", align_bytes=64)
+        neg = [sb.tile([P, PACK, P], F32, name="neg_scores0", align_bytes=64),
+               sb.tile([P, PACK, P], F32, name="neg_scores1", align_bytes=64)]
         neg_max0 = sb.tile([P, 1], F32, name="neg_max0", tag="order", align_bytes=64)
         neg_max = sb.tile([P, 1], F32, name="neg_max")
-        nc.vector.tensor_scalar(neg[:, 0], scores[0][:].rearrange("q (s t) -> q t s", t=PACK), -1.0, None,
+        nc.vector.tensor_scalar(neg[0][:], scores[0][:].rearrange("q (s t) -> q t s", t=PACK), -1.0, None,
                                 op0=ALU.mult, op1=ALU.min, accum_out=neg_max0[:])
-        nc.vector.tensor_scalar(neg[:, 1], scores[1][:].rearrange("q (s t) -> q t s", t=PACK), -1.0, neg_max0[:],
+        nc.vector.tensor_scalar(neg[1][:], scores[1][:].rearrange("q (s t) -> q t s", t=PACK), -1.0, neg_max0[:],
                                 op0=ALU.mult, op1=ALU.min, accum_out=neg_max[:])
 
         v_codes = sb.tile([P, PAGES * DV], U32, name="v_codes", tag="order", align_bytes=64)
@@ -132,10 +135,10 @@ def tile_attend_pkv4_soft_kernel(tc, qT, k_words, k_scales, v_words, v_scales, v
 
         prob = sb.tile([P, N], F32, name="prob", align_bytes=64)
         sums = sb.tile([P, N // EXP_COLS], F32, name="sums")
-        neg_flat = neg[:].rearrange("q g t s -> q (g t s)")
         for c in range(N // EXP_COLS):
             cs = slice(c * EXP_COLS, (c + 1) * EXP_COLS)
-            nc.scalar.activation(prob[:, cs], neg_flat[:, cs], ACT.Exp, bias=neg_max[:], scale=-1.0,
+            g, c0 = divmod(c * EXP_COLS, PAGE)
+            nc.scalar.activation(prob[:, cs], neg[g][:].rearrange("q t s -> q (t s)")[:, c0:c0 + EXP_COLS], ACT.Exp, bias=neg_max[:], scale=-1.0,
                                  accum_out=sums[:, c:c + 1])
 
         y = ps.tile([P, DV], F32, name="y")
@@ -145,7 +148,7 @@ def tile_attend_pkv4_soft_kernel(tc, qT, k_words, k_scales, v_words, v_scales, v
             for t in range(PACK):
                 c0 = g * PAGE + t * P
                 nc.tensor.transpose(turned[:, t, :], prob[:, c0:c0 + P], ident[:])
-            w = sb.tile([P, NQ, PACK], BF16, name="w_bf%d" % g, align_bytes=64)
+            w = sb.tile([P, NQ, PACK], BF16, name="w_bf%d" % g, tag="w_bf%d" % g, align_bytes=64)
             nc.vector.tensor_tensor(w[:], turned[:].rearrange("s t q -> s q t"),
                                     vs_cols[g][:].unsqueeze(1).to_broadcast([P, NQ, PACK]), ALU.mult)
             w_bf.append(w)

@@ -25,7 +25,19 @@ FP4X4 = mybir.dt.float4_e2m1fn_x4
 ALU = mybir.AluOpType
 ACT = mybir.ActivationFunctionType
 EXP_COLS = 256
-VS_AT = 4 * PASSES * PACK * NQ
+K_FIRST = 512
+
+KS_AT = 0
+IDENT_AT = 1536
+VSCALE_AT = 2048
+VS_AT = T
+V_AT = VS_AT
+W_AT = V_AT - 512
+PAIRS_AT = VS_AT + 2 * T
+K_AT = VS_AT + 4 * T
+LAST_WORDS_AT = K_AT + 4 * T + 2048
+PROB_AT = LAST_WORDS_AT + 1024
+QBF_AT = PROB_AT + 4 * N
 
 
 def tile_attend_pkv4_soft_kernel(tc, qT, k_words, k_scales, v_words, v_scales, vs, offs, voffs, out):
@@ -39,34 +51,25 @@ def tile_attend_pkv4_soft_kernel(tc, qT, k_words, k_scales, v_words, v_scales, v
         k_list = lists.tile([P, N // 16], U16, name="k_list")
         v_list = lists.tile([P, PAGES * DV // 16], U16, name="v_list")
 
-        k_scale_pool = sb.tile([P, T], U8, name="k_scale_pool", tag="q_codes", align_bytes=64)
+        k_scale_pool = shared.tile([P, T], U8, name="k_scale_pool", align_bytes=64, offset=KS_AT)
         vs_pool = shared.tile([P, T], F32, name="vs_pool", align_bytes=64, offset=VS_AT)
-        k_pool = sb.tile([P, T], I32, name="k_pool", align_bytes=64)
-        v_pool = sb.tile([P, POOL_PAGES * DV], I32, name="v_pool", tag="w_bf0", align_bytes=64)
-        q_raw = shared.tile([P, PASSES, PACK, NQ], F32, name="q_raw", align_bytes=64, offset=0)
+        k_pool = shared.tile([P, T], I32, name="k_pool", align_bytes=64, offset=K_AT)
+        q_raw = sb.tile([P, PASSES, PACK, NQ], F32, name="q_raw", align_bytes=64)
+        k_planes = sb.tile([P, PASSES * N], U8, name="k_planes", align_bytes=64)
 
         nc.vector.memset(k_scale_pool[:].bitcast(I32), 0)
         nc.vector.memset(vs_pool[:].bitcast(I32), 0)
+        nc.vector.memset(k_planes[:].bitcast(I32), 0)
 
+        k_rows = k_words[0].rearrange("g t b -> g (t b)").bitcast(I32)
         nc.sync.dma_start(k_list[:], offs)
         nc.sync.dma_start(v_list[:], voffs)
+        nc.sync.dma_start(k_pool[:, :K_FIRST], k_rows[:, :K_FIRST])
         nc.sync.dma_start(k_scale_pool[:].bitcast(I32)[0:P:4, :], k_scales.bitcast(I32).rearrange("o f c -> (o f) c"))
         nc.sync.dma_start(q_raw[:].rearrange("p o j w -> p o (j w)"),
                           qT[0].rearrange("(o p j) w -> p o (j w)", o=PASSES, j=PACK))
-        nc.sync.dma_start(k_pool[:], k_words[0].rearrange("g t b -> g (t b)").bitcast(I32))
+        nc.sync.dma_start(k_pool[:, K_FIRST:], k_rows[:, K_FIRST:])
         nc.scalar.dma_start(vs_pool[0:1, :], vs[0:1, :])
-
-        q_bf = sb.tile([P, PASSES, NQ, PACK], BF16, name="q_bf", tag="ident", align_bytes=64)
-        nc.scalar.copy(q_bf[:], q_raw[:].rearrange("p o j w -> p o w j"))
-
-        v_scale_pool = shared.tile([P, POOL_PAGES * DV], U8, name="v_scale_pool", align_bytes=64, offset=0)
-        k_planes = shared.tile([P, PASSES * N], U8, name="k_planes", align_bytes=64, offset=POOL_PAGES * DV)
-        nc.gpsimd.memset(v_scale_pool[:].bitcast(I32), 0)
-        nc.gpsimd.memset(k_planes[:].bitcast(I32), 0)
-        v_scale_rows = v_scales.bitcast(I32).rearrange("u (a r) c -> r a u c", r=4)
-        for r in range(4):
-            nc.sync.dma_start(
-                v_scale_pool[:].bitcast(I32)[r:P:32, :].rearrange("p (u c) -> p u c", u=POOL_PAGES), v_scale_rows[r])
 
         k_scale_rows = sb.tile([P, N], U8, name="k_scale_rows", align_bytes=64)
         nc.vector.tensor_copy(k_scale_rows[:], k_scale_pool[:].indirect(k_list[:]))
@@ -74,40 +77,47 @@ def tile_attend_pkv4_soft_kernel(tc, qT, k_words, k_scales, v_words, v_scales, v
             for r in range(4):
                 nc.sync.dma_start(k_planes[:].bitcast(I32)[r:P:32, o * N // 4:(o + 1) * N // 4],
                                   k_scale_rows[:].bitcast(I32)[64 * o + 4 * r:64 * (o + 1):16, :])
-        nc.sync.dma_start(v_pool[:].rearrange("g (u e) -> g u e", u=POOL_PAGES),
-                          v_words.rearrange("u g e r -> g u (e r)").bitcast(I32))
 
-        q_codes = sb.tile([P, PASSES * NQ], U32, name="q_codes", tag="q_codes", align_bytes=64)
-        q_scale = sb.tile([P, PASSES * NQ], U8, name="q_scale", align_bytes=64)
-        nc.vector.quantize_mx(out=q_codes[:].bitcast(FP8X4), scales=q_scale[:],
-                              in_=q_bf[:].rearrange("p o w j -> p (o w j)"))
-        ident = sb.tile([P, P], F32, name="ident", tag="ident", align_bytes=64)
+        q_bf = shared.tile([P, PASSES, NQ, PACK], BF16, name="q_bf", align_bytes=64, offset=QBF_AT)
+        nc.scalar.copy(q_bf[:], q_raw[:].rearrange("p o j w -> p o w j"))
+
+        ident = shared.tile([P, P], F32, name="ident", align_bytes=64, offset=IDENT_AT)
         make_identity(nc, ident[:])
+        v_scale_pool = shared.tile([P, POOL_PAGES * DV], U8, name="v_scale_pool", align_bytes=64, offset=VSCALE_AT)
+        nc.gpsimd.memset(v_scale_pool[:].bitcast(I32), 0)
+        v_scale_rows = v_scales.bitcast(I32).rearrange("u (a r) c -> r a u c", r=4)
+        for r in range(4):
+            nc.sync.dma_start(
+                v_scale_pool[:].bitcast(I32)[r:P:32, :].rearrange("p (u c) -> p u c", u=POOL_PAGES), v_scale_rows[r])
 
         vs_row = sb.tile([P, N], F32, name="vs_row", align_bytes=64)
         nc.vector.tensor_copy(vs_row[:], vs_pool[:].indirect(k_list[:]))
+        v_pool = shared.tile([P, POOL_PAGES * DV], I32, name="v_pool", align_bytes=64, offset=V_AT)
+        nc.sync.dma_start(v_pool[:].rearrange("g (u e) -> g u e", u=POOL_PAGES),
+                          v_words.rearrange("u g e r -> g u (e r)").bitcast(I32))
         vs_cols = []
         for g in range(PAGES):
-            turned = ps.tile([P, PACK, P], F32, name="vs_turned%d" % g, tag="bank%d" % g)
-            for t in range(PACK):
-                nc.tensor.transpose(turned[:, t, :], vs_row[:, g * PAGE + t:(g + 1) * PAGE:PACK], ident[:])
             cols = sb.tile([P, PACK], F32, name="vs_cols%d" % g)
-            nc.scalar.copy(cols[:], turned[:, :, 0])
+            nc.scalar.dma_start(cols[:], vs_row[0:1, g * PAGE:(g + 1) * PAGE].rearrange("o (s t) -> o s t", t=PACK))
             vs_cols.append(cols)
 
-
+        q_codes = shared.tile([P, PASSES * NQ], U32, name="q_codes", align_bytes=64, offset=PAIRS_AT + 4 * PAGE)
+        q_scale = sb.tile([P, PASSES * NQ], U8, name="q_scale", align_bytes=64)
         scores = []
-        k_pairs = []
         for g in range(PAGES):
-            pairs = shared.tile([P, PAGE], U32, name="k_pairs%d" % g, align_bytes=64, offset=VS_AT + 4 * PAGE * g)
+            pairs = shared.tile([P, PAGE], U32, name="k_pairs%d" % g, align_bytes=64, offset=(PAIRS_AT, QBF_AT)[g])
             nc.vector.tensor_copy(pairs[:], k_pool[:].bitcast(U32).indirect(
                 k_list[:, g * PAGE // 16:(g + 1) * PAGE // 16]))
-            k_pairs.append(pairs)
-        for g in range(PAGES):
-            halves = k_pairs[g][:].bitcast(U16).rearrange("p (n o) -> p o n", o=PASSES)
-            score = ps.tile([P, PAGE], F32, name="score%d" % g, tag="bank%d" % g)
+            if g == 0:
+                nc.vector.quantize_mx(out=q_codes[:].bitcast(FP8X4), scales=q_scale[:],
+                                      in_=q_bf[:].rearrange("p o w j -> p (o w j)"))
+            halves = pairs[:].bitcast(U16).rearrange("p (n o) -> p o n", o=PASSES)
+            score = ps.tile([P, PAGE], F32, name="score%d" % g)
             for o in range(PASSES):
-                words = sb.tile([P, PAGE], U16, name="k_words%d_%d" % (g, o), align_bytes=64)
+                if (g, o) == (PAGES - 1, PASSES - 1):
+                    words = shared.tile([P, PAGE], U16, name="k_words_last", align_bytes=64, offset=LAST_WORDS_AT)
+                else:
+                    words = sb.tile([P, PAGE], U16, name="k_words%d_%d" % (g, o), align_bytes=64)
                 nc.vector.tensor_copy(words[:], halves[:, o, :])
                 nc.tensor.matmul_mx(
                     out=score[:],
@@ -118,28 +128,30 @@ def tile_attend_pkv4_soft_kernel(tc, qT, k_words, k_scales, v_words, v_scales, v
                     start=(o == 0), stop=(o == PASSES - 1))
             scores.append(score)
 
-        v_plane = shared.tile([P, PAGES * DV], U8, name="v_plane", align_bytes=64, offset=VS_AT)
-        nc.vector.tensor_copy(v_plane[:], v_scale_pool[:].indirect(v_list[:]))
-
-        neg = [sb.tile([P, PACK, P], F32, name="neg_scores0", align_bytes=64),
+        neg = [shared.tile([P, PACK, P], F32, name="neg_scores0", align_bytes=64, offset=K_AT),
                sb.tile([P, PACK, P], F32, name="neg_scores1", align_bytes=64)]
-        neg_max0 = sb.tile([P, 1], F32, name="neg_max0", tag="order", align_bytes=64)
+        neg_max0 = sb.tile([P, 1], F32, name="neg_max0")
         neg_max = sb.tile([P, 1], F32, name="neg_max")
         nc.vector.tensor_scalar(neg[0][:], scores[0][:].rearrange("q (s t) -> q t s", t=PACK), -1.0, None,
                                 op0=ALU.mult, op1=ALU.min, accum_out=neg_max0[:])
         nc.vector.tensor_scalar(neg[1][:], scores[1][:].rearrange("q (s t) -> q t s", t=PACK), -1.0, neg_max0[:],
                                 op0=ALU.mult, op1=ALU.min, accum_out=neg_max[:])
 
-        v_codes = sb.tile([P, PAGES * DV], U32, name="v_codes", tag="order", align_bytes=64)
+        v_codes = shared.tile([P, PAGES * DV], U32, name="v_codes", align_bytes=64, offset=LAST_WORDS_AT - 1536)
+        v_plane = shared.tile([P, PAGES * DV], U8, name="v_plane", align_bytes=64, offset=LAST_WORDS_AT + 512)
+        nc.vector.tensor_copy(v_plane[:], v_scale_pool[:].indirect(v_list[:]))
         nc.vector.tensor_copy(v_codes[:], v_pool[:].bitcast(U32).indirect(v_list[:]))
 
-        prob = sb.tile([P, N], F32, name="prob", align_bytes=64)
+        prob = shared.tile([P, N], F32, name="prob", align_bytes=64, offset=PROB_AT)
         sums = sb.tile([P, N // EXP_COLS], F32, name="sums")
         for c in range(N // EXP_COLS):
             cs = slice(c * EXP_COLS, (c + 1) * EXP_COLS)
             g, c0 = divmod(c * EXP_COLS, PAGE)
             nc.scalar.activation(prob[:, cs], neg[g][:].rearrange("q t s -> q (t s)")[:, c0:c0 + EXP_COLS], ACT.Exp, bias=neg_max[:], scale=-1.0,
                                  accum_out=sums[:, c:c + 1])
+        sums_again = sb.tile([P, N // EXP_COLS], F32, name="sums_again")
+        total = sb.tile([P, 1], F32, name="total")
+        nc.scalar.activation(sums_again[:], sums[:], ACT.Copy, accum_out=total[:])
 
         y = ps.tile([P, DV], F32, name="y")
         w_bf = []
@@ -148,12 +160,12 @@ def tile_attend_pkv4_soft_kernel(tc, qT, k_words, k_scales, v_words, v_scales, v
             for t in range(PACK):
                 c0 = g * PAGE + t * P
                 nc.tensor.transpose(turned[:, t, :], prob[:, c0:c0 + P], ident[:])
-            w = sb.tile([P, NQ, PACK], BF16, name="w_bf%d" % g, tag="w_bf%d" % g, align_bytes=64)
+            w = shared.tile([P, NQ, PACK], BF16, name="w_bf%d" % g, align_bytes=64, offset=W_AT + 2 * PAGE * g)
             nc.vector.tensor_tensor(w[:], turned[:].rearrange("s t q -> s q t"),
                                     vs_cols[g][:].unsqueeze(1).to_broadcast([P, NQ, PACK]), ALU.mult)
             w_bf.append(w)
         for g in range(PAGES):
-            w_codes = sb.tile([P, NQ], U32, name="w_codes%d" % g, align_bytes=64)
+            w_codes = shared.tile([P, NQ], U32, name="w_codes%d" % g, align_bytes=64, offset=PROB_AT + 4 * NQ * g)
             w_scale = sb.tile([P, NQ], U8, name="w_scale%d" % g, align_bytes=64)
             nc.vector.quantize_mx(out=w_codes[:].bitcast(FP8X4), scales=w_scale[:],
                                   in_=w_bf[g][:].rearrange("s q t -> s (q t)"))
@@ -163,9 +175,7 @@ def tile_attend_pkv4_soft_kernel(tc, qT, k_words, k_scales, v_words, v_scales, v
                 rhs_scale=v_plane[:, g * DV:(g + 1) * DV],
                 start=(g == 0), stop=(g == PAGES - 1))
 
-        total = sb.tile([P, 1], F32, name="total")
-        nc.vector.tensor_reduce(total[:], sums[:], mybir.AxisListType.X, ALU.add)
-        inv = sb.tile([P, 1], F32, name="inv")
+        inv = shared.tile([P, 1], F32, name="inv", align_bytes=64, offset=W_AT + 4 * PAGE)
         nc.vector.reciprocal(inv[:], total[:])
         res = sb.tile([P, DV], F32, name="res", align_bytes=64)
         nc.vector.tensor_scalar(res[:], y[:], inv[:], None, op0=ALU.mult)

@@ -55,11 +55,12 @@ def tile_attend_pkv4_soft_kernel(tc, qT, k_words, k_scales, v_words, v_scales, v
         vs_pool = shared.tile([P, T], F32, name="vs_pool", align_bytes=64, offset=VS_AT)
         k_pool = shared.tile([P, T], I32, name="k_pool", align_bytes=64, offset=K_AT)
         q_raw = sb.tile([P, PASSES, PACK, NQ], F32, name="q_raw", align_bytes=64)
-        k_planes = sb.tile([P, PASSES * N], U8, name="k_planes", align_bytes=64)
+        k_planes = [sb.tile([P, N], U8, name="k_plane%d" % o, align_bytes=64) for o in range(PASSES)]
 
         nc.vector.memset(k_scale_pool[:].bitcast(I32), 0)
         nc.vector.memset(vs_pool[:].bitcast(I32), 0)
-        nc.vector.memset(k_planes[:].bitcast(I32), 0)
+        for o in range(PASSES):
+            nc.vector.memset(k_planes[o][:].bitcast(I32), 0)
 
         k_rows = k_words[0].rearrange("g t b -> g (t b)").bitcast(I32)
         nc.sync.dma_start(k_list[:], offs)
@@ -75,7 +76,7 @@ def tile_attend_pkv4_soft_kernel(tc, qT, k_words, k_scales, v_words, v_scales, v
         nc.vector.tensor_copy(k_scale_rows[:], k_scale_pool[:].indirect(k_list[:]))
         for o in range(PASSES):
             for r in range(4):
-                nc.sync.dma_start(k_planes[:].bitcast(I32)[r:P:32, o * N // 4:(o + 1) * N // 4],
+                nc.sync.dma_start(k_planes[o][:].bitcast(I32)[r:P:32, :],
                                   k_scale_rows[:].bitcast(I32)[64 * o + 4 * r:64 * (o + 1):16, :])
 
         q_bf = shared.tile([P, PASSES, NQ, PACK], BF16, name="q_bf", align_bytes=64, offset=QBF_AT)
@@ -113,8 +114,9 @@ def tile_attend_pkv4_soft_kernel(tc, qT, k_words, k_scales, v_words, v_scales, v
                                       in_=q_bf[:].rearrange("p o w j -> p (o w j)"))
             halves = pairs[:].bitcast(U16).rearrange("p (n o) -> p o n", o=PASSES)
             score = ps.tile([P, PAGE], F32, name="score%d" % g)
-            for o in range(PASSES):
-                if (g, o) == (PAGES - 1, PASSES - 1):
+            order = ((0, 1), (1, 0))[g]
+            for o in order:
+                if (g, o) == (PAGES - 1, order[-1]):
                     words = shared.tile([P, PAGE], U16, name="k_words_last", align_bytes=64, offset=LAST_WORDS_AT)
                 else:
                     words = sb.tile([P, PAGE], U16, name="k_words%d_%d" % (g, o), align_bytes=64)
@@ -124,8 +126,8 @@ def tile_attend_pkv4_soft_kernel(tc, qT, k_words, k_scales, v_words, v_scales, v
                     lhsT=q_codes[:, o * NQ:(o + 1) * NQ].bitcast(FP8X4),
                     lhsT_scale=q_scale[:, o * NQ:(o + 1) * NQ],
                     rhs=words[:].bitcast(FP4X4),
-                    rhs_scale=k_planes[:, o * N + g * PAGE:o * N + (g + 1) * PAGE],
-                    start=(o == 0), stop=(o == PASSES - 1))
+                    rhs_scale=k_planes[o][:, g * PAGE:(g + 1) * PAGE],
+                    start=(o == order[0]), stop=(o == order[-1]))
             scores.append(score)
 
         neg = [shared.tile([P, PACK, P], F32, name="neg_scores0", align_bytes=64, offset=K_AT),
@@ -153,7 +155,7 @@ def tile_attend_pkv4_soft_kernel(tc, qT, k_words, k_scales, v_words, v_scales, v
         total = sb.tile([P, 1], F32, name="total")
         nc.scalar.activation(sums_again[:], sums[:], ACT.Copy, accum_out=total[:])
 
-        y = ps.tile([P, DV], F32, name="y")
+        y = [ps.tile([P, DV // 2], F32, name="y%d" % h) for h in range(2)]
         w_bf = []
         for g in range(PAGES):
             turned = ps.tile([P, PACK, NQ], F32, name="p_turned%d" % g)
@@ -169,14 +171,17 @@ def tile_attend_pkv4_soft_kernel(tc, qT, k_words, k_scales, v_words, v_scales, v
             w_scale = sb.tile([P, NQ], U8, name="w_scale%d" % g, align_bytes=64)
             nc.vector.quantize_mx(out=w_codes[:].bitcast(FP8X4), scales=w_scale[:],
                                   in_=w_bf[g][:].rearrange("s q t -> s (q t)"))
-            nc.tensor.matmul_mx(
-                out=y[:], lhsT=w_codes[:].bitcast(FP8X4), lhsT_scale=w_scale[:],
-                rhs=v_codes[:, g * DV:(g + 1) * DV].bitcast(FP8X4),
-                rhs_scale=v_plane[:, g * DV:(g + 1) * DV],
-                start=(g == 0), stop=(g == PAGES - 1))
+            for h in range(2):
+                cols = slice(g * DV + h * P, g * DV + (h + 1) * P)
+                nc.tensor.matmul_mx(
+                    out=y[h][:], lhsT=w_codes[:].bitcast(FP8X4), lhsT_scale=w_scale[:],
+                    rhs=v_codes[:, cols].bitcast(FP8X4), rhs_scale=v_plane[:, cols],
+                    start=(g == 0), stop=(g == PAGES - 1))
 
         inv = shared.tile([P, 1], F32, name="inv", align_bytes=64, offset=W_AT + 4 * PAGE)
         nc.vector.reciprocal(inv[:], total[:])
-        res = sb.tile([P, DV], F32, name="res", align_bytes=64)
-        nc.vector.tensor_scalar(res[:], y[:], inv[:], None, op0=ALU.mult)
-        nc.sync.dma_start(out[0], res[:])
+        res = [sb.tile([P, DV // 2], F32, name="res%d" % h, align_bytes=64) for h in range(2)]
+        nc.vector.tensor_scalar(res[0][:], y[0][:], inv[:], None, op0=ALU.mult)
+        nc.sync.dma_start(out[0][:, :P], res[0][:])
+        nc.scalar.activation(res[1][:], y[1][:], ACT.Copy, scale=inv[:])
+        nc.scalar.dma_start(out[0][:, P:], res[1][:])

@@ -10,6 +10,7 @@ PACK = 4
 PAGES = N // PAGE
 POOL_PAGES = T // PAGE
 PASSES = D // PAGE
+QUADS = 4
 
 FLOPS = 2 * NQ * N * (D + DV)
 BYTES = 4 * D * NQ + 4 * P * T + PASSES * 16 * T + 4 * P * POOL_PAGES * DV + POOL_PAGES * 16 * DV + 4 * T + 2 * P * (N + PAGES * DV) // 16 + 4 * NQ * DV
@@ -25,19 +26,13 @@ FP4X4 = mybir.dt.float4_e2m1fn_x4
 ALU = mybir.AluOpType
 ACT = mybir.ActivationFunctionType
 EXP_COLS = 256
-K_FIRST = 512
+K_FIRST = 1024
+VS_CLEARED = 2048
 
-KS_AT = 0
-IDENT_AT = 1536
-VSCALE_AT = 2048
-VS_AT = T
-V_AT = VS_AT
-W_AT = V_AT - 512
-PAIRS_AT = VS_AT + 2 * T
-K_AT = VS_AT + 4 * T
-LAST_WORDS_AT = K_AT + 4 * T + 2048
-PROB_AT = LAST_WORDS_AT + 1024
-QBF_AT = PROB_AT + 4 * N
+PAIRS_AT = 0
+WORDS_AT = PAIRS_AT + 4 * N
+V_AT = WORDS_AT + 4 * N
+COLS_AT = V_AT + 4 * POOL_PAGES * DV
 
 
 def tile_attend_pkv4_soft_kernel(tc, qT, k_words, k_scales, v_words, v_scales, vs, offs, voffs, out):
@@ -51,87 +46,91 @@ def tile_attend_pkv4_soft_kernel(tc, qT, k_words, k_scales, v_words, v_scales, v
         k_list = lists.tile([P, N // 16], U16, name="k_list")
         v_list = lists.tile([P, PAGES * DV // 16], U16, name="v_list")
 
-        k_scale_pool = shared.tile([P, T], U8, name="k_scale_pool", align_bytes=64, offset=KS_AT)
-        vs_pool = shared.tile([P, T], F32, name="vs_pool", align_bytes=64, offset=VS_AT)
-        k_pool = shared.tile([P, T], I32, name="k_pool", align_bytes=64, offset=K_AT)
+        k_scale_pool = sb.tile([P, T], U8, name="k_scale_pool", align_bytes=64)
+        v_scale_pool = sb.tile([P, POOL_PAGES * DV], U8, name="v_scale_pool", align_bytes=64)
+        vs_pool = sb.tile([P, T], F32, name="vs_pool", align_bytes=64)
+        k_pool = sb.tile([P, T], I32, name="k_pool", align_bytes=64)
         q_raw = sb.tile([P, PASSES, PACK, NQ], F32, name="q_raw", align_bytes=64)
-        k_planes = [sb.tile([P, N], U8, name="k_plane%d" % o, align_bytes=64) for o in range(PASSES)]
+        k_planes = sb.tile([P, PASSES * N], U8, name="k_planes", align_bytes=64)
+        v_plane = sb.tile([P, PAGES * DV], U8, name="v_plane", align_bytes=64)
 
         nc.vector.memset(k_scale_pool[:].bitcast(I32), 0)
-        nc.vector.memset(vs_pool[:].bitcast(I32), 0)
-        for o in range(PASSES):
-            nc.vector.memset(k_planes[o][:].bitcast(I32), 0)
+        nc.vector.memset(v_scale_pool[:].bitcast(I32), 0)
+        nc.vector.memset(vs_pool[:, :VS_CLEARED].bitcast(I32), 0)
+        nc.vector.memset(k_planes[:].bitcast(I32), 0)
+        nc.vector.memset(v_plane[:].bitcast(I32), 0)
 
         k_rows = k_words[0].rearrange("g t b -> g (t b)").bitcast(I32)
         nc.sync.dma_start(k_list[:], offs)
         nc.sync.dma_start(v_list[:], voffs)
         nc.sync.dma_start(k_pool[:, :K_FIRST], k_rows[:, :K_FIRST])
-        nc.sync.dma_start(k_scale_pool[:].bitcast(I32)[0:P:4, :], k_scales.bitcast(I32).rearrange("o f c -> (o f) c"))
+        nc.sync.dma_start(k_scale_pool[:].bitcast(I32)[0:P:4, :], k_scales.bitcast(I32).rearrange("o f c -> f o c"))
+        nc.sync.dma_start(v_scale_pool[:].bitcast(I32)[0:P:8, :].rearrange("f (u c) -> f u c", u=POOL_PAGES),
+                          v_scales.bitcast(I32).rearrange("u f c -> f u c"))
+        nc.sync.dma_start(k_pool[:, K_FIRST:], k_rows[:, K_FIRST:])
         nc.sync.dma_start(q_raw[:].rearrange("p o j w -> p o (j w)"),
                           qT[0].rearrange("(o p j) w -> p o (j w)", o=PASSES, j=PACK))
-        nc.sync.dma_start(k_pool[:, K_FIRST:], k_rows[:, K_FIRST:])
-        nc.scalar.dma_start(vs_pool[0:1, :], vs[0:1, :])
+        nc.scalar.dma_start(vs_pool[0:1, :VS_CLEARED], vs[0:1, :VS_CLEARED])
 
         k_scale_rows = sb.tile([P, N], U8, name="k_scale_rows", align_bytes=64)
         nc.vector.tensor_copy(k_scale_rows[:], k_scale_pool[:].indirect(k_list[:]))
-        for o in range(PASSES):
-            for r in range(4):
-                nc.sync.dma_start(k_planes[o][:].bitcast(I32)[r:P:32, :],
-                                  k_scale_rows[:].bitcast(I32)[64 * o + 4 * r:64 * (o + 1):16, :])
-
-        q_bf = shared.tile([P, PASSES, NQ, PACK], BF16, name="q_bf", align_bytes=64, offset=QBF_AT)
-        nc.scalar.copy(q_bf[:], q_raw[:].rearrange("p o j w -> p o w j"))
-
-        ident = shared.tile([P, P], F32, name="ident", align_bytes=64, offset=IDENT_AT)
-        make_identity(nc, ident[:])
-        v_scale_pool = shared.tile([P, POOL_PAGES * DV], U8, name="v_scale_pool", align_bytes=64, offset=VSCALE_AT)
-        nc.gpsimd.memset(v_scale_pool[:].bitcast(I32), 0)
-        v_scale_rows = v_scales.bitcast(I32).rearrange("u (a r) c -> r a u c", r=4)
-        for r in range(4):
-            nc.sync.dma_start(
-                v_scale_pool[:].bitcast(I32)[r:P:32, :].rearrange("p (u c) -> p u c", u=POOL_PAGES), v_scale_rows[r])
-
-        vs_row = sb.tile([P, N], F32, name="vs_row", align_bytes=64)
-        nc.vector.tensor_copy(vs_row[:], vs_pool[:].indirect(k_list[:]))
+        for a in range(QUADS):
+            if a == QUADS // 2:
+                nc.sync.dma_start(vs_pool[:, VS_CLEARED:], vs[:, VS_CLEARED:])
+            nc.sync.dma_start(k_planes[:].bitcast(I32)[32 * a:32 * a + 4, :].rearrange("r (o c) -> r o c", o=PASSES),
+                              k_scale_rows[:].bitcast(I32)[32 * a:32 * (a + 1):4, :])
         v_pool = shared.tile([P, POOL_PAGES * DV], I32, name="v_pool", align_bytes=64, offset=V_AT)
         nc.sync.dma_start(v_pool[:].rearrange("g (u e) -> g u e", u=POOL_PAGES),
                           v_words.rearrange("u g e r -> g u (e r)").bitcast(I32))
-        vs_cols = []
-        for g in range(PAGES):
-            cols = sb.tile([P, PACK], F32, name="vs_cols%d" % g)
-            nc.scalar.dma_start(cols[:], vs_row[0:1, g * PAGE:(g + 1) * PAGE].rearrange("o (s t) -> o s t", t=PACK))
-            vs_cols.append(cols)
+        v_scale_rows = sb.tile([P, PAGES * DV], U8, name="v_scale_rows", align_bytes=64)
+        nc.vector.tensor_copy(v_scale_rows[:], v_scale_pool[:].indirect(v_list[:]))
+        for a in range(QUADS):
+            nc.sync.dma_start(v_plane[:].bitcast(I32)[32 * a:32 * a + 4, :],
+                              v_scale_rows[:].bitcast(I32)[32 * a:32 * (a + 1):8, :])
 
-        q_codes = shared.tile([P, PASSES * NQ], U32, name="q_codes", align_bytes=64, offset=PAIRS_AT + 4 * PAGE)
+        q_bf = sb.tile([P, PASSES, NQ, PACK], BF16, name="q_bf", align_bytes=64)
+        nc.scalar.copy(q_bf[:], q_raw[:].rearrange("p o j w -> p o w j"))
+
+        pairs = []
+        for g in range(PAGES):
+            both = shared.tile([P, PAGE], U32, name="k_pairs%d" % g, align_bytes=64, offset=PAIRS_AT + 4 * PAGE * g)
+            nc.vector.tensor_copy(both[:], k_pool[:].bitcast(U32).indirect(
+                k_list[:, g * PAGE // 16:(g + 1) * PAGE // 16]))
+            pairs.append(both)
+        words = []
+        for g in range(PAGES):
+            parted = shared.tile([P, PASSES, PAGE], U16, name="k_words%d" % g, align_bytes=64, offset=WORDS_AT + 4 * PAGE * g)
+            nc.vector.tensor_copy(parted[:], pairs[g][:].bitcast(U16).rearrange("p (n o) -> p o n", o=PASSES))
+            words.append(parted)
+        q_codes = sb.tile([P, PASSES * NQ], U32, name="q_codes", align_bytes=64)
         q_scale = sb.tile([P, PASSES * NQ], U8, name="q_scale", align_bytes=64)
+        nc.vector.quantize_mx(out=q_codes[:].bitcast(FP8X4), scales=q_scale[:],
+                              in_=q_bf[:].rearrange("p o w j -> p (o w j)"))
         scores = []
         for g in range(PAGES):
-            pairs = shared.tile([P, PAGE], U32, name="k_pairs%d" % g, align_bytes=64, offset=(PAIRS_AT, QBF_AT)[g])
-            nc.vector.tensor_copy(pairs[:], k_pool[:].bitcast(U32).indirect(
-                k_list[:, g * PAGE // 16:(g + 1) * PAGE // 16]))
-            if g == 0:
-                nc.vector.quantize_mx(out=q_codes[:].bitcast(FP8X4), scales=q_scale[:],
-                                      in_=q_bf[:].rearrange("p o w j -> p (o w j)"))
-            halves = pairs[:].bitcast(U16).rearrange("p (n o) -> p o n", o=PASSES)
             score = ps.tile([P, PAGE], F32, name="score%d" % g)
-            order = ((0, 1), (1, 0))[g]
-            for o in order:
-                if (g, o) == (PAGES - 1, order[-1]):
-                    words = shared.tile([P, PAGE], U16, name="k_words_last", align_bytes=64, offset=LAST_WORDS_AT)
-                else:
-                    words = sb.tile([P, PAGE], U16, name="k_words%d_%d" % (g, o), align_bytes=64)
-                nc.vector.tensor_copy(words[:], halves[:, o, :])
+            for o in range(PASSES):
                 nc.tensor.matmul_mx(
                     out=score[:],
                     lhsT=q_codes[:, o * NQ:(o + 1) * NQ].bitcast(FP8X4),
                     lhsT_scale=q_scale[:, o * NQ:(o + 1) * NQ],
-                    rhs=words[:].bitcast(FP4X4),
-                    rhs_scale=k_planes[o][:, g * PAGE:(g + 1) * PAGE],
-                    start=(o == order[0]), stop=(o == order[-1]))
+                    rhs=words[g][:, o, :].bitcast(FP4X4),
+                    rhs_scale=k_planes[:, o * N + g * PAGE:o * N + (g + 1) * PAGE],
+                    start=(o == 0), stop=(o == PASSES - 1))
             scores.append(score)
 
-        neg = [shared.tile([P, PACK, P], F32, name="neg_scores0", align_bytes=64, offset=K_AT),
-               sb.tile([P, PACK, P], F32, name="neg_scores1", align_bytes=64)]
+        vs_row = sb.tile([P, N], F32, name="vs_row", align_bytes=64)
+        nc.vector.tensor_copy(vs_row[:], vs_pool[:].indirect(k_list[:]))
+        vs_cols = []
+        for g in range(PAGES):
+            cols = shared.tile([P, PACK], F32, name="vs_cols%d" % g, align_bytes=64, offset=COLS_AT + 64 * g)
+            nc.sync.dma_start(cols[:], vs_row[0:1, g * PAGE:(g + 1) * PAGE].rearrange("o (s t) -> o s t", t=PACK))
+            vs_cols.append(cols)
+
+        ident = shared.tile([P, P], F32, name="ident", align_bytes=64, offset=PAIRS_AT + 4 * PAGE)
+        make_identity(nc, ident[:])
+
+        neg = [sb.tile([P, PACK, P], F32, name="neg_scores%d" % g, align_bytes=64) for g in range(PAGES)]
         neg_max0 = sb.tile([P, 1], F32, name="neg_max0")
         neg_max = sb.tile([P, 1], F32, name="neg_max")
         nc.vector.tensor_scalar(neg[0][:], scores[0][:].rearrange("q (s t) -> q t s", t=PACK), -1.0, None,
@@ -139,12 +138,10 @@ def tile_attend_pkv4_soft_kernel(tc, qT, k_words, k_scales, v_words, v_scales, v
         nc.vector.tensor_scalar(neg[1][:], scores[1][:].rearrange("q (s t) -> q t s", t=PACK), -1.0, neg_max0[:],
                                 op0=ALU.mult, op1=ALU.min, accum_out=neg_max[:])
 
-        v_codes = shared.tile([P, PAGES * DV], U32, name="v_codes", align_bytes=64, offset=LAST_WORDS_AT - 1536)
-        v_plane = shared.tile([P, PAGES * DV], U8, name="v_plane", align_bytes=64, offset=LAST_WORDS_AT + 512)
-        nc.vector.tensor_copy(v_plane[:], v_scale_pool[:].indirect(v_list[:]))
+        v_codes = shared.tile([P, PAGES * DV], U32, name="v_codes", align_bytes=64, offset=WORDS_AT + 4 * PAGE)
         nc.vector.tensor_copy(v_codes[:], v_pool[:].bitcast(U32).indirect(v_list[:]))
 
-        prob = shared.tile([P, N], F32, name="prob", align_bytes=64, offset=PROB_AT)
+        prob = sb.tile([P, N], F32, name="prob", align_bytes=64)
         sums = sb.tile([P, N // EXP_COLS], F32, name="sums")
         for c in range(N // EXP_COLS):
             cs = slice(c * EXP_COLS, (c + 1) * EXP_COLS)
@@ -162,12 +159,12 @@ def tile_attend_pkv4_soft_kernel(tc, qT, k_words, k_scales, v_words, v_scales, v
             for t in range(PACK):
                 c0 = g * PAGE + t * P
                 nc.tensor.transpose(turned[:, t, :], prob[:, c0:c0 + P], ident[:])
-            w = shared.tile([P, NQ, PACK], BF16, name="w_bf%d" % g, align_bytes=64, offset=W_AT + 2 * PAGE * g)
+            w = shared.tile([P, NQ, PACK], BF16, name="w_bf%d" % g, align_bytes=64, offset=V_AT + 2 * PAGE * g)
             nc.vector.tensor_tensor(w[:], turned[:].rearrange("s t q -> s q t"),
                                     vs_cols[g][:].unsqueeze(1).to_broadcast([P, NQ, PACK]), ALU.mult)
             w_bf.append(w)
         for g in range(PAGES):
-            w_codes = shared.tile([P, NQ], U32, name="w_codes%d" % g, align_bytes=64, offset=PROB_AT + 4 * NQ * g)
+            w_codes = sb.tile([P, NQ], U32, name="w_codes%d" % g, align_bytes=64)
             w_scale = sb.tile([P, NQ], U8, name="w_scale%d" % g, align_bytes=64)
             nc.vector.quantize_mx(out=w_codes[:].bitcast(FP8X4), scales=w_scale[:],
                                   in_=w_bf[g][:].rearrange("s q t -> s (q t)"))
@@ -178,7 +175,7 @@ def tile_attend_pkv4_soft_kernel(tc, qT, k_words, k_scales, v_words, v_scales, v
                     rhs=v_codes[:, cols].bitcast(FP8X4), rhs_scale=v_plane[:, cols],
                     start=(g == 0), stop=(g == PAGES - 1))
 
-        inv = shared.tile([P, 1], F32, name="inv", align_bytes=64, offset=W_AT + 4 * PAGE)
+        inv = shared.tile([P, 1], F32, name="inv", align_bytes=64, offset=COLS_AT + 64 * (PAGES - 1))
         nc.vector.reciprocal(inv[:], total[:])
         res = [sb.tile([P, DV // 2], F32, name="res%d" % h, align_bytes=64) for h in range(2)]
         nc.vector.tensor_scalar(res[0][:], y[0][:], inv[:], None, op0=ALU.mult)

@@ -27,7 +27,6 @@ ALU = mybir.AluOpType
 ACT = mybir.ActivationFunctionType
 EXP_COLS = 256
 K_FIRST = 1024
-VS_CLEARED = 2048
 
 PAIRS_AT = 0
 WORDS_AT = PAIRS_AT + 4 * N
@@ -56,7 +55,7 @@ def tile_attend_pkv4_soft_kernel(tc, qT, k_words, k_scales, v_words, v_scales, v
 
         nc.vector.memset(k_scale_pool[:].bitcast(I32), 0)
         nc.vector.memset(v_scale_pool[:].bitcast(I32), 0)
-        nc.vector.memset(vs_pool[:, :VS_CLEARED].bitcast(I32), 0)
+        nc.vector.memset(vs_pool[:].bitcast(I32), 0)
         nc.vector.memset(k_planes[:].bitcast(I32), 0)
         nc.vector.memset(v_plane[:].bitcast(I32), 0)
 
@@ -70,13 +69,12 @@ def tile_attend_pkv4_soft_kernel(tc, qT, k_words, k_scales, v_words, v_scales, v
         nc.sync.dma_start(k_pool[:, K_FIRST:], k_rows[:, K_FIRST:])
         nc.sync.dma_start(q_raw[:].rearrange("p o j w -> p o (j w)"),
                           qT[0].rearrange("(o p j) w -> p o (j w)", o=PASSES, j=PACK))
-        nc.scalar.dma_start(vs_pool[0:1, :VS_CLEARED], vs[0:1, :VS_CLEARED])
 
         k_scale_rows = sb.tile([P, N], U8, name="k_scale_rows", align_bytes=64)
         nc.vector.tensor_copy(k_scale_rows[:], k_scale_pool[:].indirect(k_list[:]))
         for a in range(QUADS):
             if a == QUADS // 2:
-                nc.sync.dma_start(vs_pool[:, VS_CLEARED:], vs[:, VS_CLEARED:])
+                nc.sync.dma_start(vs_pool[0:1, :], vs[0:1, :])
             nc.sync.dma_start(k_planes[:].bitcast(I32)[32 * a:32 * a + 4, :].rearrange("r (o c) -> r o c", o=PASSES),
                               k_scale_rows[:].bitcast(I32)[32 * a:32 * (a + 1):4, :])
         v_pool = shared.tile([P, POOL_PAGES * DV], I32, name="v_pool", align_bytes=64, offset=V_AT)
@@ -119,12 +117,12 @@ def tile_attend_pkv4_soft_kernel(tc, qT, k_words, k_scales, v_words, v_scales, v
                     start=(o == 0), stop=(o == PASSES - 1))
             scores.append(score)
 
-        vs_row = sb.tile([P, N], F32, name="vs_row", align_bytes=64)
-        nc.vector.tensor_copy(vs_row[:], vs_pool[:].indirect(k_list[:]))
         vs_cols = []
         for g in range(PAGES):
+            vs_row = sb.tile([P, PAGE], F32, name="vs_row%d" % g, align_bytes=64)
+            nc.vector.tensor_copy(vs_row[:], vs_pool[:].indirect(k_list[:, g * PAGE // 16:(g + 1) * PAGE // 16]))
             cols = shared.tile([P, PACK], F32, name="vs_cols%d" % g, align_bytes=64, offset=COLS_AT + 64 * g)
-            nc.sync.dma_start(cols[:], vs_row[0:1, g * PAGE:(g + 1) * PAGE].rearrange("o (s t) -> o s t", t=PACK))
+            nc.sync.dma_start(cols[:], vs_row[0:1, :].rearrange("o (s t) -> o s t", t=PACK))
             vs_cols.append(cols)
 
         ident = shared.tile([P, P], F32, name="ident", align_bytes=64, offset=PAIRS_AT + 4 * PAGE)

@@ -27,6 +27,7 @@ ALU = mybir.AluOpType
 ACT = mybir.ActivationFunctionType
 EXP_COLS = 256
 K_FIRST = 1024
+VS_WIDE = 128
 
 PAIRS_AT = 0
 WORDS_AT = PAIRS_AT + 4 * N
@@ -55,14 +56,13 @@ def tile_attend_pkv4_soft_kernel(tc, qT, k_words, k_scales, v_words, v_scales, v
 
         nc.vector.memset(k_scale_pool[:].bitcast(I32), 0)
         nc.vector.memset(v_scale_pool[:].bitcast(I32), 0)
-        nc.vector.memset(vs_pool[:].bitcast(I32), 0)
         nc.vector.memset(k_planes[:].bitcast(I32), 0)
         nc.vector.memset(v_plane[:].bitcast(I32), 0)
 
         k_rows = k_words[0].rearrange("g t b -> g (t b)").bitcast(I32)
+        nc.sync.dma_start(k_pool[:, :K_FIRST], k_rows[:, :K_FIRST])
         nc.sync.dma_start(k_list[:], offs)
         nc.sync.dma_start(v_list[:], voffs)
-        nc.sync.dma_start(k_pool[:, :K_FIRST], k_rows[:, :K_FIRST])
         nc.sync.dma_start(k_scale_pool[:].bitcast(I32)[0:P:4, :], k_scales.bitcast(I32).rearrange("o f c -> f o c"))
         nc.sync.dma_start(v_scale_pool[:].bitcast(I32)[0:P:8, :].rearrange("f (u c) -> f u c", u=POOL_PAGES),
                           v_scales.bitcast(I32).rearrange("u f c -> f u c"))
@@ -70,11 +70,16 @@ def tile_attend_pkv4_soft_kernel(tc, qT, k_words, k_scales, v_words, v_scales, v
         nc.sync.dma_start(q_raw[:].rearrange("p o j w -> p o (j w)"),
                           qT[0].rearrange("(o p j) w -> p o (j w)", o=PASSES, j=PACK))
 
+        vs_head = sb.tile([P, VS_WIDE], F32, name="vs_head", align_bytes=64)
+        nc.scalar.dma_start(vs_head[:], vs[:, :VS_WIDE])
+        nc.scalar.activation(vs_pool[:].rearrange("p (a c) -> p a c", c=VS_WIDE),
+                             vs_head[:].unsqueeze(1).to_broadcast([P, T // VS_WIDE, VS_WIDE]), ACT.Copy)
+
         k_scale_rows = sb.tile([P, N], U8, name="k_scale_rows", align_bytes=64)
         nc.vector.tensor_copy(k_scale_rows[:], k_scale_pool[:].indirect(k_list[:]))
         for a in range(QUADS):
             if a == QUADS // 2:
-                nc.sync.dma_start(vs_pool[0:1, :], vs[0:1, :])
+                nc.sync.dma_start(vs_pool[0:1, VS_WIDE:], vs[0:1, VS_WIDE:])
             nc.sync.dma_start(k_planes[:].bitcast(I32)[32 * a:32 * a + 4, :].rearrange("r (o c) -> r o c", o=PASSES),
                               k_scale_rows[:].bitcast(I32)[32 * a:32 * (a + 1):4, :])
         v_pool = shared.tile([P, POOL_PAGES * DV], I32, name="v_pool", align_bytes=64, offset=V_AT)

@@ -28,6 +28,7 @@ ACT = mybir.ActivationFunctionType
 EXP_COLS = 256
 K_FIRST = 1024
 VS_WIDE = 128
+VS_FILLED = 3072
 
 PAIRS_AT = 0
 WORDS_AT = PAIRS_AT + 4 * N
@@ -50,7 +51,7 @@ def tile_attend_pkv4_soft_kernel(tc, qT, k_words, k_scales, v_words, v_scales, v
         v_scale_pool = sb.tile([P, POOL_PAGES * DV], U8, name="v_scale_pool", align_bytes=64)
         vs_pool = sb.tile([P, T], F32, name="vs_pool", align_bytes=64)
         k_pool = sb.tile([P, T], I32, name="k_pool", align_bytes=64)
-        q_raw = sb.tile([P, PASSES, PACK, NQ], F32, name="q_raw", align_bytes=64)
+        q_raw = shared.tile([P, PASSES, PACK, NQ], F32, name="q_raw", align_bytes=64, offset=WORDS_AT)
         k_planes = sb.tile([P, PASSES * N], U8, name="k_planes", align_bytes=64)
         v_plane = sb.tile([P, PAGES * DV], U8, name="v_plane", align_bytes=64)
 
@@ -58,6 +59,7 @@ def tile_attend_pkv4_soft_kernel(tc, qT, k_words, k_scales, v_words, v_scales, v
         nc.vector.memset(v_scale_pool[:].bitcast(I32), 0)
         nc.vector.memset(k_planes[:].bitcast(I32), 0)
         nc.vector.memset(v_plane[:].bitcast(I32), 0)
+        nc.vector.memset(vs_pool[:, VS_FILLED:].bitcast(I32), 0)
 
         k_rows = k_words[0].rearrange("g t b -> g (t b)").bitcast(I32)
         nc.sync.dma_start(k_pool[:, :K_FIRST], k_rows[:, :K_FIRST])
@@ -72,8 +74,8 @@ def tile_attend_pkv4_soft_kernel(tc, qT, k_words, k_scales, v_words, v_scales, v
 
         vs_head = sb.tile([P, VS_WIDE], F32, name="vs_head", align_bytes=64)
         nc.scalar.dma_start(vs_head[:], vs[:, :VS_WIDE])
-        nc.scalar.activation(vs_pool[:].rearrange("p (a c) -> p a c", c=VS_WIDE),
-                             vs_head[:].unsqueeze(1).to_broadcast([P, T // VS_WIDE, VS_WIDE]), ACT.Copy)
+        nc.scalar.activation(vs_pool[:, :VS_FILLED].rearrange("p (a c) -> p a c", c=VS_WIDE),
+                             vs_head[:].unsqueeze(1).to_broadcast([P, VS_FILLED // VS_WIDE, VS_WIDE]), ACT.Copy)
 
         k_scale_rows = sb.tile([P, N], U8, name="k_scale_rows", align_bytes=64)
         nc.vector.tensor_copy(k_scale_rows[:], k_scale_pool[:].indirect(k_list[:]))
@@ -100,15 +102,15 @@ def tile_attend_pkv4_soft_kernel(tc, qT, k_words, k_scales, v_words, v_scales, v
             nc.vector.tensor_copy(both[:], k_pool[:].bitcast(U32).indirect(
                 k_list[:, g * PAGE // 16:(g + 1) * PAGE // 16]))
             pairs.append(both)
+        q_codes = sb.tile([P, PASSES * NQ], U32, name="q_codes", align_bytes=64)
+        q_scale = sb.tile([P, PASSES * NQ], U8, name="q_scale", align_bytes=64)
+        nc.vector.quantize_mx(out=q_codes[:].bitcast(FP8X4), scales=q_scale[:],
+                              in_=q_bf[:].rearrange("p o w j -> p (o w j)"))
         words = []
         for g in range(PAGES):
             parted = shared.tile([P, PASSES, PAGE], U16, name="k_words%d" % g, align_bytes=64, offset=WORDS_AT + 4 * PAGE * g)
             nc.vector.tensor_copy(parted[:], pairs[g][:].bitcast(U16).rearrange("p (n o) -> p o n", o=PASSES))
             words.append(parted)
-        q_codes = sb.tile([P, PASSES * NQ], U32, name="q_codes", align_bytes=64)
-        q_scale = sb.tile([P, PASSES * NQ], U8, name="q_scale", align_bytes=64)
-        nc.vector.quantize_mx(out=q_codes[:].bitcast(FP8X4), scales=q_scale[:],
-                              in_=q_bf[:].rearrange("p o w j -> p (o w j)"))
         scores = []
         for g in range(PAGES):
             score = ps.tile([P, PAGE], F32, name="score%d" % g)
@@ -122,24 +124,22 @@ def tile_attend_pkv4_soft_kernel(tc, qT, k_words, k_scales, v_words, v_scales, v
                     start=(o == 0), stop=(o == PASSES - 1))
             scores.append(score)
 
+        neg = [sb.tile([P, PACK, P], F32, name="neg_scores%d" % g, align_bytes=64) for g in range(PAGES)]
+        neg_maxes = [sb.tile([P, 1], F32, name="neg_max%d" % g) for g in range(PAGES)]
         vs_cols = []
         for g in range(PAGES):
-            vs_row = sb.tile([P, PAGE], F32, name="vs_row%d" % g, align_bytes=64)
+            vs_row = shared.tile([P, PAGE], F32, name="vs_row%d" % g, align_bytes=64, offset=(PAIRS_AT, WORDS_AT)[g])
             nc.vector.tensor_copy(vs_row[:], vs_pool[:].indirect(k_list[:, g * PAGE // 16:(g + 1) * PAGE // 16]))
             cols = shared.tile([P, PACK], F32, name="vs_cols%d" % g, align_bytes=64, offset=COLS_AT + 64 * g)
             nc.sync.dma_start(cols[:], vs_row[0:1, :].rearrange("o (s t) -> o s t", t=PACK))
             vs_cols.append(cols)
+            nc.vector.tensor_scalar(neg[g][:], scores[g][:].rearrange("q (s t) -> q t s", t=PACK), -1.0,
+                                    neg_maxes[g - 1][:] if g else None,
+                                    op0=ALU.mult, op1=ALU.min, accum_out=neg_maxes[g][:])
+        neg_max = neg_maxes[-1]
 
         ident = shared.tile([P, P], F32, name="ident", align_bytes=64, offset=PAIRS_AT + 4 * PAGE)
         make_identity(nc, ident[:])
-
-        neg = [sb.tile([P, PACK, P], F32, name="neg_scores%d" % g, align_bytes=64) for g in range(PAGES)]
-        neg_max0 = sb.tile([P, 1], F32, name="neg_max0")
-        neg_max = sb.tile([P, 1], F32, name="neg_max")
-        nc.vector.tensor_scalar(neg[0][:], scores[0][:].rearrange("q (s t) -> q t s", t=PACK), -1.0, None,
-                                op0=ALU.mult, op1=ALU.min, accum_out=neg_max0[:])
-        nc.vector.tensor_scalar(neg[1][:], scores[1][:].rearrange("q (s t) -> q t s", t=PACK), -1.0, neg_max0[:],
-                                op0=ALU.mult, op1=ALU.min, accum_out=neg_max[:])
 
         v_codes = shared.tile([P, PAGES * DV], U32, name="v_codes", align_bytes=64, offset=WORDS_AT + 4 * PAGE)
         nc.vector.tensor_copy(v_codes[:], v_pool[:].bitcast(U32).indirect(v_list[:]))

@@ -28,11 +28,11 @@ ACT = mybir.ActivationFunctionType
 EXP_COLS = 256
 K_FIRST = 1024
 VS_WIDE = 128
-VS_FILLED = 3072
+VS_FILLED = 2048
 
 PAIRS_AT = 0
 WORDS_AT = PAIRS_AT + 4 * N
-V_AT = WORDS_AT + 4 * N
+V_AT = WORDS_AT + 4 * N + 1024
 COLS_AT = V_AT + 4 * POOL_PAGES * DV
 
 
@@ -51,7 +51,8 @@ def tile_attend_pkv4_soft_kernel(tc, qT, k_words, k_scales, v_words, v_scales, v
         v_scale_pool = sb.tile([P, POOL_PAGES * DV], U8, name="v_scale_pool", align_bytes=64)
         vs_pool = sb.tile([P, T], F32, name="vs_pool", align_bytes=64)
         k_pool = sb.tile([P, T], I32, name="k_pool", align_bytes=64)
-        q_raw = shared.tile([P, PASSES, PACK, NQ], F32, name="q_raw", align_bytes=64, offset=WORDS_AT)
+        q_raw = [shared.tile([P, PACK, NQ], F32, name="q_raw%d" % o, align_bytes=64, offset=WORDS_AT + 1024 + 4 * PAGE * (PASSES - 1 - o))
+                 for o in range(PASSES)]
         k_planes = sb.tile([P, PASSES * N], U8, name="k_planes", align_bytes=64)
         v_plane = sb.tile([P, PAGES * DV], U8, name="v_plane", align_bytes=64)
 
@@ -69,21 +70,22 @@ def tile_attend_pkv4_soft_kernel(tc, qT, k_words, k_scales, v_words, v_scales, v
         nc.sync.dma_start(v_scale_pool[:].bitcast(I32)[0:P:8, :].rearrange("f (u c) -> f u c", u=POOL_PAGES),
                           v_scales.bitcast(I32).rearrange("u f c -> f u c"))
         nc.sync.dma_start(k_pool[:, K_FIRST:], k_rows[:, K_FIRST:])
-        nc.sync.dma_start(q_raw[:].rearrange("p o j w -> p o (j w)"),
-                          qT[0].rearrange("(o p j) w -> p o (j w)", o=PASSES, j=PACK))
+        q_rows = qT[0].rearrange("(o p j) w -> o p (j w)", o=PASSES, j=PACK)
+        for o in range(PASSES):
+            nc.sync.dma_start(q_raw[o][:].rearrange("p j w -> p (j w)"), q_rows[o])
+        nc.sync.dma_start(vs_pool[0:1, VS_FILLED:], vs[0:1, VS_FILLED:])
 
         vs_head = sb.tile([P, VS_WIDE], F32, name="vs_head", align_bytes=64)
         nc.scalar.dma_start(vs_head[:], vs[:, :VS_WIDE])
         nc.scalar.activation(vs_pool[:, :VS_FILLED].rearrange("p (a c) -> p a c", c=VS_WIDE),
                              vs_head[:].unsqueeze(1).to_broadcast([P, VS_FILLED // VS_WIDE, VS_WIDE]), ACT.Copy)
+        nc.scalar.dma_start(vs_pool[0:1, VS_WIDE:VS_FILLED], vs[0:1, VS_WIDE:VS_FILLED])
 
         k_scale_rows = sb.tile([P, N], U8, name="k_scale_rows", align_bytes=64)
         nc.vector.tensor_copy(k_scale_rows[:], k_scale_pool[:].indirect(k_list[:]))
         for a in range(QUADS):
-            if a == QUADS // 2:
-                nc.sync.dma_start(vs_pool[0:1, VS_WIDE:], vs[0:1, VS_WIDE:])
-            nc.sync.dma_start(k_planes[:].bitcast(I32)[32 * a:32 * a + 4, :].rearrange("r (o c) -> r o c", o=PASSES),
-                              k_scale_rows[:].bitcast(I32)[32 * a:32 * (a + 1):4, :])
+            nc.scalar.dma_start(k_planes[:].bitcast(I32)[32 * a:32 * a + 4, :].rearrange("r (o c) -> r o c", o=PASSES),
+                                k_scale_rows[:].bitcast(I32)[32 * a:32 * (a + 1):4, :])
         v_pool = shared.tile([P, POOL_PAGES * DV], I32, name="v_pool", align_bytes=64, offset=V_AT)
         nc.sync.dma_start(v_pool[:].rearrange("g (u e) -> g u e", u=POOL_PAGES),
                           v_words.rearrange("u g e r -> g u (e r)").bitcast(I32))
@@ -94,7 +96,8 @@ def tile_attend_pkv4_soft_kernel(tc, qT, k_words, k_scales, v_words, v_scales, v
                               v_scale_rows[:].bitcast(I32)[32 * a:32 * (a + 1):8, :])
 
         q_bf = sb.tile([P, PASSES, NQ, PACK], BF16, name="q_bf", align_bytes=64)
-        nc.scalar.copy(q_bf[:], q_raw[:].rearrange("p o j w -> p o w j"))
+        for o in range(PASSES):
+            nc.scalar.copy(q_bf[:, o], q_raw[o][:].rearrange("p j w -> p w j"))
 
         pairs = []
         for g in range(PAGES):
@@ -102,6 +105,13 @@ def tile_attend_pkv4_soft_kernel(tc, qT, k_words, k_scales, v_words, v_scales, v
             nc.vector.tensor_copy(both[:], k_pool[:].bitcast(U32).indirect(
                 k_list[:, g * PAGE // 16:(g + 1) * PAGE // 16]))
             pairs.append(both)
+
+        def token_scales(g, vs_row):
+            nc.vector.tensor_copy(vs_row[:], vs_pool[:].indirect(k_list[:, g * PAGE // 16:(g + 1) * PAGE // 16]))
+            cols = shared.tile([P, PACK], F32, name="vs_cols%d" % g, align_bytes=64, offset=COLS_AT + 64 * g)
+            nc.scalar.dma_start(cols[:], vs_row[0:1, :].rearrange("o (s t) -> o s t", t=PACK))
+            return cols
+
         q_codes = sb.tile([P, PASSES * NQ], U32, name="q_codes", align_bytes=64)
         q_scale = sb.tile([P, PASSES * NQ], U8, name="q_scale", align_bytes=64)
         nc.vector.quantize_mx(out=q_codes[:].bitcast(FP8X4), scales=q_scale[:],
@@ -126,13 +136,9 @@ def tile_attend_pkv4_soft_kernel(tc, qT, k_words, k_scales, v_words, v_scales, v
 
         neg = [sb.tile([P, PACK, P], F32, name="neg_scores%d" % g, align_bytes=64) for g in range(PAGES)]
         neg_maxes = [sb.tile([P, 1], F32, name="neg_max%d" % g) for g in range(PAGES)]
-        vs_cols = []
+        vs_cols = [token_scales(0, shared.tile([P, PAGE], F32, name="vs_row0", align_bytes=64, offset=PAIRS_AT)),
+                   token_scales(1, sb.tile([P, PAGE], F32, name="vs_row1", align_bytes=64))]
         for g in range(PAGES):
-            vs_row = shared.tile([P, PAGE], F32, name="vs_row%d" % g, align_bytes=64, offset=(PAIRS_AT, WORDS_AT)[g])
-            nc.vector.tensor_copy(vs_row[:], vs_pool[:].indirect(k_list[:, g * PAGE // 16:(g + 1) * PAGE // 16]))
-            cols = shared.tile([P, PACK], F32, name="vs_cols%d" % g, align_bytes=64, offset=COLS_AT + 64 * g)
-            nc.sync.dma_start(cols[:], vs_row[0:1, :].rearrange("o (s t) -> o s t", t=PACK))
-            vs_cols.append(cols)
             nc.vector.tensor_scalar(neg[g][:], scores[g][:].rearrange("q (s t) -> q t s", t=PACK), -1.0,
                                     neg_maxes[g - 1][:] if g else None,
                                     op0=ALU.mult, op1=ALU.min, accum_out=neg_maxes[g][:])

@@ -25,15 +25,13 @@ FP8X4 = mybir.dt.float8_e4m3fn_x4
 FP4X4 = mybir.dt.float4_e2m1fn_x4
 ALU = mybir.AluOpType
 ACT = mybir.ActivationFunctionType
-EXP_COLS = 256
-K_FIRST = 1024
-VS_WIDE = 128
+K_FIRST = 768
+VS_WIDE = 32
 VS_FILLED = 2048
 
 PAIRS_AT = 0
 WORDS_AT = PAIRS_AT + 4 * N
-V_AT = WORDS_AT + 4 * N + 1024
-COLS_AT = V_AT + 4 * POOL_PAGES * DV
+COLS_AT = WORDS_AT + 4 * N + 1024
 
 
 def tile_attend_pkv4_soft_kernel(tc, qT, k_words, k_scales, v_words, v_scales, vs, offs, voffs, out):
@@ -86,7 +84,7 @@ def tile_attend_pkv4_soft_kernel(tc, qT, k_words, k_scales, v_words, v_scales, v
         for a in range(QUADS):
             nc.scalar.dma_start(k_planes[:].bitcast(I32)[32 * a:32 * a + 4, :].rearrange("r (o c) -> r o c", o=PASSES),
                                 k_scale_rows[:].bitcast(I32)[32 * a:32 * (a + 1):4, :])
-        v_pool = shared.tile([P, POOL_PAGES * DV], I32, name="v_pool", align_bytes=64, offset=V_AT)
+        v_pool = sb.tile([P, POOL_PAGES * DV], I32, name="v_pool", align_bytes=64)
         nc.sync.dma_start(v_pool[:].rearrange("g (u e) -> g u e", u=POOL_PAGES),
                           v_words.rearrange("u g e r -> g u (e r)").bitcast(I32))
         v_scale_rows = sb.tile([P, PAGES * DV], U8, name="v_scale_rows", align_bytes=64)
@@ -136,9 +134,10 @@ def tile_attend_pkv4_soft_kernel(tc, qT, k_words, k_scales, v_words, v_scales, v
 
         neg = [sb.tile([P, PACK, P], F32, name="neg_scores%d" % g, align_bytes=64) for g in range(PAGES)]
         neg_maxes = [sb.tile([P, 1], F32, name="neg_max%d" % g) for g in range(PAGES)]
-        vs_cols = [token_scales(0, shared.tile([P, PAGE], F32, name="vs_row0", align_bytes=64, offset=PAIRS_AT)),
-                   token_scales(1, sb.tile([P, PAGE], F32, name="vs_row1", align_bytes=64))]
+        vs_cols = []
         for g in range(PAGES):
+            vs_cols.append(token_scales(g, shared.tile([P, PAGE], F32, name="vs_row%d" % g, align_bytes=64,
+                                                       offset=(PAIRS_AT, WORDS_AT)[g])))
             nc.vector.tensor_scalar(neg[g][:], scores[g][:].rearrange("q (s t) -> q t s", t=PACK), -1.0,
                                     neg_maxes[g - 1][:] if g else None,
                                     op0=ALU.mult, op1=ALU.min, accum_out=neg_maxes[g][:])
@@ -151,15 +150,13 @@ def tile_attend_pkv4_soft_kernel(tc, qT, k_words, k_scales, v_words, v_scales, v
         nc.vector.tensor_copy(v_codes[:], v_pool[:].bitcast(U32).indirect(v_list[:]))
 
         prob = sb.tile([P, N], F32, name="prob", align_bytes=64)
-        sums = sb.tile([P, N // EXP_COLS], F32, name="sums")
-        for c in range(N // EXP_COLS):
-            cs = slice(c * EXP_COLS, (c + 1) * EXP_COLS)
-            g, c0 = divmod(c * EXP_COLS, PAGE)
-            nc.scalar.activation(prob[:, cs], neg[g][:].rearrange("q t s -> q (t s)")[:, c0:c0 + EXP_COLS], ACT.Exp, bias=neg_max[:], scale=-1.0,
-                                 accum_out=sums[:, c:c + 1])
-        sums_again = sb.tile([P, N // EXP_COLS], F32, name="sums_again")
+        for g in range(PAGES):
+            for t in range(PACK):
+                c0 = g * PAGE + t * P
+                nc.scalar.activation(prob[:, c0:c0 + P], neg[g][:, t, :], ACT.Exp, bias=neg_max[:], scale=-1.0)
+        prob_again = sb.tile([P, N], F32, name="prob_again", align_bytes=64)
         total = sb.tile([P, 1], F32, name="total")
-        nc.scalar.activation(sums_again[:], sums[:], ACT.Copy, accum_out=total[:])
+        nc.scalar.activation(prob_again[:], prob[:], ACT.Copy, accum_out=total[:])
 
         y = [ps.tile([P, DV // 2], F32, name="y%d" % h) for h in range(2)]
         w_bf = []
@@ -168,7 +165,7 @@ def tile_attend_pkv4_soft_kernel(tc, qT, k_words, k_scales, v_words, v_scales, v
             for t in range(PACK):
                 c0 = g * PAGE + t * P
                 nc.tensor.transpose(turned[:, t, :], prob[:, c0:c0 + P], ident[:])
-            w = shared.tile([P, NQ, PACK], BF16, name="w_bf%d" % g, align_bytes=64, offset=V_AT + 2 * PAGE * g)
+            w = sb.tile([P, NQ, PACK], BF16, name="w_bf%d" % g, align_bytes=64)
             nc.vector.tensor_tensor(w[:], turned[:].rearrange("s t q -> s q t"),
                                     vs_cols[g][:].unsqueeze(1).to_broadcast([P, NQ, PACK]), ALU.mult)
             w_bf.append(w)

@@ -134,10 +134,9 @@ def tile_attend_pkv4_soft_kernel(tc, qT, k_words, k_scales, v_words, v_scales, v
 
         neg = [sb.tile([P, PACK, P], F32, name="neg_scores%d" % g, align_bytes=64) for g in range(PAGES)]
         neg_maxes = [sb.tile([P, 1], F32, name="neg_max%d" % g) for g in range(PAGES)]
-        vs_cols = []
+        vs_cols = [token_scales(0, shared.tile([P, PAGE], F32, name="vs_row0", align_bytes=64, offset=PAIRS_AT)),
+                   token_scales(1, sb.tile([P, PAGE], F32, name="vs_row1", align_bytes=64))]
         for g in range(PAGES):
-            vs_cols.append(token_scales(g, shared.tile([P, PAGE], F32, name="vs_row%d" % g, align_bytes=64,
-                                                       offset=(PAIRS_AT, WORDS_AT)[g])))
             nc.vector.tensor_scalar(neg[g][:], scores[g][:].rearrange("q (s t) -> q t s", t=PACK), -1.0,
                                     neg_maxes[g - 1][:] if g else None,
                                     op0=ALU.mult, op1=ALU.min, accum_out=neg_maxes[g][:])

@@ -32,6 +32,7 @@ VS_FILLED = 2048
 PAIRS_AT = 0
 WORDS_AT = PAIRS_AT + 4 * N
 COLS_AT = WORDS_AT + 4 * N + 1024
+VS_AT = COLS_AT + 64 * PAGES
 
 
 def tile_attend_pkv4_soft_kernel(tc, qT, k_words, k_scales, v_words, v_scales, vs, offs, voffs, out):
@@ -47,7 +48,7 @@ def tile_attend_pkv4_soft_kernel(tc, qT, k_words, k_scales, v_words, v_scales, v
 
         k_scale_pool = sb.tile([P, T], U8, name="k_scale_pool", align_bytes=64)
         v_scale_pool = sb.tile([P, POOL_PAGES * DV], U8, name="v_scale_pool", align_bytes=64)
-        vs_pool = sb.tile([P, T], F32, name="vs_pool", align_bytes=64)
+        vs_pool = shared.tile([P, T], F32, name="vs_pool", align_bytes=64, offset=VS_AT)
         k_pool = sb.tile([P, T], I32, name="k_pool", align_bytes=64)
         q_raw = [shared.tile([P, PACK, NQ], F32, name="q_raw%d" % o, align_bytes=64, offset=WORDS_AT + 1024 + 4 * PAGE * (PASSES - 1 - o))
                  for o in range(PASSES)]
@@ -142,7 +143,7 @@ def tile_attend_pkv4_soft_kernel(tc, qT, k_words, k_scales, v_words, v_scales, v
                                     op0=ALU.mult, op1=ALU.min, accum_out=neg_maxes[g][:])
         neg_max = neg_maxes[-1]
 
-        ident = shared.tile([P, P], F32, name="ident", align_bytes=64, offset=PAIRS_AT + 4 * PAGE)
+        ident = shared.tile([P, P], F32, name="ident", align_bytes=64, offset=VS_AT)
         make_identity(nc, ident[:])
 
         v_codes = shared.tile([P, PAGES * DV], U32, name="v_codes", align_bytes=64, offset=WORDS_AT + 4 * PAGE)

@@ -27,12 +27,16 @@ ALU = mybir.AluOpType
 ACT = mybir.ActivationFunctionType
 K_FIRST = 768
 VS_WIDE = 32
-VS_FILLED = 2048
+VS_FILLED = 2816
 
 PAIRS_AT = 0
 WORDS_AT = PAIRS_AT + 4 * N
-COLS_AT = WORDS_AT + 4 * N + 1024
-VS_AT = COLS_AT + 64 * PAGES
+V_CODES_AT = WORDS_AT + 4 * PAGE - 64
+V_AT = WORDS_AT + 4 * N
+COLS_AT = V_AT + 4 * POOL_PAGES * DV
+ROWS_AT = COLS_AT + 64 * PAGES
+QBF_AT = ROWS_AT + 2 * PAGE
+VS_AT = ROWS_AT + 4 * N
 
 
 def tile_attend_pkv4_soft_kernel(tc, qT, k_words, k_scales, v_words, v_scales, vs, offs, voffs, out):
@@ -50,8 +54,8 @@ def tile_attend_pkv4_soft_kernel(tc, qT, k_words, k_scales, v_words, v_scales, v
         v_scale_pool = sb.tile([P, POOL_PAGES * DV], U8, name="v_scale_pool", align_bytes=64)
         vs_pool = shared.tile([P, T], F32, name="vs_pool", align_bytes=64, offset=VS_AT)
         k_pool = sb.tile([P, T], I32, name="k_pool", align_bytes=64)
-        q_raw = [shared.tile([P, PACK, NQ], F32, name="q_raw%d" % o, align_bytes=64, offset=WORDS_AT + 1024 + 4 * PAGE * (PASSES - 1 - o))
-                 for o in range(PASSES)]
+        q_raw = [sb.tile([P, PACK, NQ], F32, name="q_raw0", align_bytes=64),
+                 shared.tile([P, PACK, NQ], F32, name="q_raw1", align_bytes=64, offset=V_AT - 2 * PAGE)]
         k_planes = sb.tile([P, PASSES * N], U8, name="k_planes", align_bytes=64)
         v_plane = sb.tile([P, PAGES * DV], U8, name="v_plane", align_bytes=64)
 
@@ -72,31 +76,31 @@ def tile_attend_pkv4_soft_kernel(tc, qT, k_words, k_scales, v_words, v_scales, v
         q_rows = qT[0].rearrange("(o p j) w -> o p (j w)", o=PASSES, j=PACK)
         for o in range(PASSES):
             nc.sync.dma_start(q_raw[o][:].rearrange("p j w -> p (j w)"), q_rows[o])
-        nc.sync.dma_start(vs_pool[0:1, VS_FILLED:], vs[0:1, VS_FILLED:])
 
         vs_head = sb.tile([P, VS_WIDE], F32, name="vs_head", align_bytes=64)
         nc.scalar.dma_start(vs_head[:], vs[:, :VS_WIDE])
         nc.scalar.activation(vs_pool[:, :VS_FILLED].rearrange("p (a c) -> p a c", c=VS_WIDE),
                              vs_head[:].unsqueeze(1).to_broadcast([P, VS_FILLED // VS_WIDE, VS_WIDE]), ACT.Copy)
-        nc.scalar.dma_start(vs_pool[0:1, VS_WIDE:VS_FILLED], vs[0:1, VS_WIDE:VS_FILLED])
+        nc.scalar.dma_start(vs_pool[0:1, :], vs[0:1, :])
+
+        q_bf = shared.tile([P, PASSES, NQ, PACK], BF16, name="q_bf", align_bytes=64, offset=QBF_AT)
+        for o in range(PASSES):
+            nc.scalar.copy(q_bf[:, o], q_raw[o][:].rearrange("p j w -> p w j"))
 
         k_scale_rows = sb.tile([P, N], U8, name="k_scale_rows", align_bytes=64)
         nc.vector.tensor_copy(k_scale_rows[:], k_scale_pool[:].indirect(k_list[:]))
-        for a in range(QUADS):
+        for a in (0, 2, 1, 3):
             nc.scalar.dma_start(k_planes[:].bitcast(I32)[32 * a:32 * a + 4, :].rearrange("r (o c) -> r o c", o=PASSES),
                                 k_scale_rows[:].bitcast(I32)[32 * a:32 * (a + 1):4, :])
-        v_pool = sb.tile([P, POOL_PAGES * DV], I32, name="v_pool", align_bytes=64)
-        nc.sync.dma_start(v_pool[:].rearrange("g (u e) -> g u e", u=POOL_PAGES),
-                          v_words.rearrange("u g e r -> g u (e r)").bitcast(I32))
         v_scale_rows = sb.tile([P, PAGES * DV], U8, name="v_scale_rows", align_bytes=64)
         nc.vector.tensor_copy(v_scale_rows[:], v_scale_pool[:].indirect(v_list[:]))
         for a in range(QUADS):
             nc.sync.dma_start(v_plane[:].bitcast(I32)[32 * a:32 * a + 4, :],
                               v_scale_rows[:].bitcast(I32)[32 * a:32 * (a + 1):8, :])
 
-        q_bf = sb.tile([P, PASSES, NQ, PACK], BF16, name="q_bf", align_bytes=64)
-        for o in range(PASSES):
-            nc.scalar.copy(q_bf[:, o], q_raw[o][:].rearrange("p j w -> p w j"))
+        v_pool = shared.tile([P, POOL_PAGES * DV], I32, name="v_pool", align_bytes=64, offset=V_AT)
+        nc.sync.dma_start(v_pool[:].rearrange("g (u e) -> g u e", u=POOL_PAGES),
+                          v_words.rearrange("u g e r -> g u (e r)").bitcast(I32))
 
         pairs = []
         for g in range(PAGES):
@@ -113,10 +117,11 @@ def tile_attend_pkv4_soft_kernel(tc, qT, k_words, k_scales, v_words, v_scales, v
 
         q_codes = sb.tile([P, PASSES * NQ], U32, name="q_codes", align_bytes=64)
         q_scale = sb.tile([P, PASSES * NQ], U8, name="q_scale", align_bytes=64)
-        nc.vector.quantize_mx(out=q_codes[:].bitcast(FP8X4), scales=q_scale[:],
-                              in_=q_bf[:].rearrange("p o w j -> p (o w j)"))
         words = []
         for g in range(PAGES):
+            if g == PAGES - 1:
+                nc.vector.quantize_mx(out=q_codes[:].bitcast(FP8X4), scales=q_scale[:],
+                                      in_=q_bf[:].rearrange("p o w j -> p (o w j)"))
             parted = shared.tile([P, PASSES, PAGE], U16, name="k_words%d" % g, align_bytes=64, offset=WORDS_AT + 4 * PAGE * g)
             nc.vector.tensor_copy(parted[:], pairs[g][:].bitcast(U16).rearrange("p (n o) -> p o n", o=PASSES))
             words.append(parted)
@@ -134,9 +139,10 @@ def tile_attend_pkv4_soft_kernel(tc, qT, k_words, k_scales, v_words, v_scales, v
             scores.append(score)
 
         neg = [sb.tile([P, PACK, P], F32, name="neg_scores%d" % g, align_bytes=64) for g in range(PAGES)]
-        neg_maxes = [sb.tile([P, 1], F32, name="neg_max%d" % g) for g in range(PAGES)]
-        vs_cols = [token_scales(0, shared.tile([P, PAGE], F32, name="vs_row0", align_bytes=64, offset=PAIRS_AT)),
-                   token_scales(1, sb.tile([P, PAGE], F32, name="vs_row1", align_bytes=64))]
+        neg_maxes = [shared.tile([P, 1], F32, name="neg_max0", align_bytes=64, offset=V_CODES_AT),
+                     sb.tile([P, 1], F32, name="neg_max1")]
+        vs_cols = [token_scales(g, shared.tile([P, PAGE], F32, name="vs_row%d" % g, align_bytes=64, offset=ROWS_AT + 4 * PAGE * g))
+                   for g in range(PAGES)]
         for g in range(PAGES):
             nc.vector.tensor_scalar(neg[g][:], scores[g][:].rearrange("q (s t) -> q t s", t=PACK), -1.0,
                                     neg_maxes[g - 1][:] if g else None,
@@ -146,7 +152,7 @@ def tile_attend_pkv4_soft_kernel(tc, qT, k_words, k_scales, v_words, v_scales, v
         ident = shared.tile([P, P], F32, name="ident", align_bytes=64, offset=VS_AT)
         make_identity(nc, ident[:])
 
-        v_codes = shared.tile([P, PAGES * DV], U32, name="v_codes", align_bytes=64, offset=WORDS_AT + 4 * PAGE)
+        v_codes = shared.tile([P, PAGES * DV], U32, name="v_codes", align_bytes=64, offset=V_CODES_AT)
         nc.vector.tensor_copy(v_codes[:], v_pool[:].bitcast(U32).indirect(v_list[:]))
 
         prob = sb.tile([P, N], F32, name="prob", align_bytes=64)

@@ -55,7 +55,7 @@ def tile_attend_pkv4_soft_kernel(tc, qT, k_words, k_scales, v_words, v_scales, v
         vs_pool = shared.tile([P, T], F32, name="vs_pool", align_bytes=64, offset=VS_AT)
         k_pool = sb.tile([P, T], I32, name="k_pool", align_bytes=64)
         q_raw = [sb.tile([P, PACK, NQ], F32, name="q_raw0", align_bytes=64),
-                 shared.tile([P, PACK, NQ], F32, name="q_raw1", align_bytes=64, offset=V_AT - 2 * PAGE)]
+                 shared.tile([P, PACK, NQ], F32, name="q_raw1", align_bytes=64, offset=WORDS_AT + 4 * PAGE)]
         k_planes = sb.tile([P, PASSES * N], U8, name="k_planes", align_bytes=64)
         v_plane = sb.tile([P, PAGES * DV], U8, name="v_plane", align_bytes=64)
 
@@ -81,7 +81,6 @@ def tile_attend_pkv4_soft_kernel(tc, qT, k_words, k_scales, v_words, v_scales, v
         nc.scalar.dma_start(vs_head[:], vs[:, :VS_WIDE])
         nc.scalar.activation(vs_pool[:, :VS_FILLED].rearrange("p (a c) -> p a c", c=VS_WIDE),
                              vs_head[:].unsqueeze(1).to_broadcast([P, VS_FILLED // VS_WIDE, VS_WIDE]), ACT.Copy)
-        nc.scalar.dma_start(vs_pool[0:1, :], vs[0:1, :])
 
         q_bf = shared.tile([P, PASSES, NQ, PACK], BF16, name="q_bf", align_bytes=64, offset=QBF_AT)
         for o in range(PASSES):
@@ -90,17 +89,19 @@ def tile_attend_pkv4_soft_kernel(tc, qT, k_words, k_scales, v_words, v_scales, v
         k_scale_rows = sb.tile([P, N], U8, name="k_scale_rows", align_bytes=64)
         nc.vector.tensor_copy(k_scale_rows[:], k_scale_pool[:].indirect(k_list[:]))
         for a in (0, 2, 1, 3):
-            nc.scalar.dma_start(k_planes[:].bitcast(I32)[32 * a:32 * a + 4, :].rearrange("r (o c) -> r o c", o=PASSES),
-                                k_scale_rows[:].bitcast(I32)[32 * a:32 * (a + 1):4, :])
+            if a == QUADS - 1:
+                nc.sync.dma_start(vs_pool[0:1, :], vs[0:1, :])
+            nc.sync.dma_start(k_planes[:].bitcast(I32)[32 * a:32 * a + 4, :].rearrange("r (o c) -> r o c", o=PASSES),
+                              k_scale_rows[:].bitcast(I32)[32 * a:32 * (a + 1):4, :])
+        v_pool = shared.tile([P, POOL_PAGES * DV], I32, name="v_pool", align_bytes=64, offset=V_AT)
+        nc.sync.dma_start(v_pool[:].rearrange("g (u e) -> g u e", u=POOL_PAGES),
+                          v_words.rearrange("u g e r -> g u (e r)").bitcast(I32))
         v_scale_rows = sb.tile([P, PAGES * DV], U8, name="v_scale_rows", align_bytes=64)
         nc.vector.tensor_copy(v_scale_rows[:], v_scale_pool[:].indirect(v_list[:]))
         for a in range(QUADS):
             nc.sync.dma_start(v_plane[:].bitcast(I32)[32 * a:32 * a + 4, :],
                               v_scale_rows[:].bitcast(I32)[32 * a:32 * (a + 1):8, :])
 
-        v_pool = shared.tile([P, POOL_PAGES * DV], I32, name="v_pool", align_bytes=64, offset=V_AT)
-        nc.sync.dma_start(v_pool[:].rearrange("g (u e) -> g u e", u=POOL_PAGES),
-                          v_words.rearrange("u g e r -> g u (e r)").bitcast(I32))
 
         pairs = []
         for g in range(PAGES):
@@ -171,7 +172,7 @@ def tile_attend_pkv4_soft_kernel(tc, qT, k_words, k_scales, v_words, v_scales, v
             for t in range(PACK):
                 c0 = g * PAGE + t * P
                 nc.tensor.transpose(turned[:, t, :], prob[:, c0:c0 + P], ident[:])
-            w = sb.tile([P, NQ, PACK], BF16, name="w_bf%d" % g, align_bytes=64)
+            w = shared.tile([P, NQ, PACK], BF16, name="w_bf%d" % g, align_bytes=64, offset=V_AT + 2 * PAGE * g)
             nc.vector.tensor_tensor(w[:], turned[:].rearrange("s t q -> s q t"),
                                     vs_cols[g][:].unsqueeze(1).to_broadcast([P, NQ, PACK]), ALU.mult)
             w_bf.append(w)

@@ -28,15 +28,18 @@ ACT = mybir.ActivationFunctionType
 K_FIRST = 768
 VS_WIDE = 32
 VS_FILLED = 2816
+VS_ROW = 8
+CHUNK = 256
+CHUNKS = N // CHUNK
 
-PAIRS_AT = 0
-WORDS_AT = PAIRS_AT + 4 * N
-V_CODES_AT = WORDS_AT + 4 * PAGE - 64
-V_AT = WORDS_AT + 4 * N
-COLS_AT = V_AT + 4 * POOL_PAGES * DV
-ROWS_AT = COLS_AT + 64 * PAGES
-QBF_AT = ROWS_AT + 2 * PAGE
-VS_AT = ROWS_AT + 4 * N
+KB = 1024
+PAIRS_AT = (0, KB, 3 * KB, 6 * KB)
+WORDS_AT = (2 * KB, 5 * KB, 7 * KB, 8 * KB)
+Q_RAW_AT = (3 * KB, 5 * KB + KB // 2)
+IDENT_AT = WORDS_AT[2] + KB // 2
+V_CODES_AT = WORDS_AT[3]
+COLS_AT = V_CODES_AT + 4 * PAGES * DV
+VS_AT = COLS_AT + 64 * PAGES
 
 
 def tile_attend_pkv4_soft_kernel(tc, qT, k_words, k_scales, v_words, v_scales, vs, offs, voffs, out):
@@ -54,8 +57,7 @@ def tile_attend_pkv4_soft_kernel(tc, qT, k_words, k_scales, v_words, v_scales, v
         v_scale_pool = sb.tile([P, POOL_PAGES * DV], U8, name="v_scale_pool", align_bytes=64)
         vs_pool = shared.tile([P, T], F32, name="vs_pool", align_bytes=64, offset=VS_AT)
         k_pool = sb.tile([P, T], I32, name="k_pool", align_bytes=64)
-        q_raw = [sb.tile([P, PACK, NQ], F32, name="q_raw0", align_bytes=64),
-                 shared.tile([P, PACK, NQ], F32, name="q_raw1", align_bytes=64, offset=WORDS_AT + 4 * PAGE)]
+        q_raw = [shared.tile([P, PACK, NQ], F32, name="q_raw%d" % o, align_bytes=64, offset=Q_RAW_AT[o]) for o in range(PASSES)]
         k_planes = sb.tile([P, PASSES * N], U8, name="k_planes", align_bytes=64)
         v_plane = sb.tile([P, PAGES * DV], U8, name="v_plane", align_bytes=64)
 
@@ -82,18 +84,17 @@ def tile_attend_pkv4_soft_kernel(tc, qT, k_words, k_scales, v_words, v_scales, v
         nc.scalar.activation(vs_pool[:, :VS_FILLED].rearrange("p (a c) -> p a c", c=VS_WIDE),
                              vs_head[:].unsqueeze(1).to_broadcast([P, VS_FILLED // VS_WIDE, VS_WIDE]), ACT.Copy)
 
-        q_bf = shared.tile([P, PASSES, NQ, PACK], BF16, name="q_bf", align_bytes=64, offset=QBF_AT)
+        q_bf = [sb.tile([P, NQ, PACK], BF16, name="q_bf%d" % o, align_bytes=64) for o in range(PASSES)]
         for o in range(PASSES):
-            nc.scalar.copy(q_bf[:, o], q_raw[o][:].rearrange("p j w -> p w j"))
+            nc.scalar.copy(q_bf[o][:], q_raw[o][:].rearrange("p j w -> p w j"))
 
         k_scale_rows = sb.tile([P, N], U8, name="k_scale_rows", align_bytes=64)
         nc.vector.tensor_copy(k_scale_rows[:], k_scale_pool[:].indirect(k_list[:]))
         for a in (0, 2, 1, 3):
-            if a == QUADS - 1:
-                nc.sync.dma_start(vs_pool[0:1, :], vs[0:1, :])
             nc.sync.dma_start(k_planes[:].bitcast(I32)[32 * a:32 * a + 4, :].rearrange("r (o c) -> r o c", o=PASSES),
                               k_scale_rows[:].bitcast(I32)[32 * a:32 * (a + 1):4, :])
-        v_pool = shared.tile([P, POOL_PAGES * DV], I32, name="v_pool", align_bytes=64, offset=V_AT)
+        nc.sync.dma_start(vs_pool[VS_ROW:VS_ROW + 1, :], vs[0:1, :])
+        v_pool = sb.tile([P, POOL_PAGES * DV], I32, name="v_pool", align_bytes=64)
         nc.sync.dma_start(v_pool[:].rearrange("g (u e) -> g u e", u=POOL_PAGES),
                           v_words.rearrange("u g e r -> g u (e r)").bitcast(I32))
         v_scale_rows = sb.tile([P, PAGES * DV], U8, name="v_scale_rows", align_bytes=64)
@@ -102,61 +103,72 @@ def tile_attend_pkv4_soft_kernel(tc, qT, k_words, k_scales, v_words, v_scales, v
             nc.sync.dma_start(v_plane[:].bitcast(I32)[32 * a:32 * a + 4, :],
                               v_scale_rows[:].bitcast(I32)[32 * a:32 * (a + 1):8, :])
 
-
-        pairs = []
+        vs_cols = []
         for g in range(PAGES):
-            both = shared.tile([P, PAGE], U32, name="k_pairs%d" % g, align_bytes=64, offset=PAIRS_AT + 4 * PAGE * g)
-            nc.vector.tensor_copy(both[:], k_pool[:].bitcast(U32).indirect(
-                k_list[:, g * PAGE // 16:(g + 1) * PAGE // 16]))
-            pairs.append(both)
-
-        def token_scales(g, vs_row):
-            nc.vector.tensor_copy(vs_row[:], vs_pool[:].indirect(k_list[:, g * PAGE // 16:(g + 1) * PAGE // 16]))
+            vs_row = sb.tile([P, PAGE], F32, name="vs_row%d" % g, align_bytes=64)
+            nc.scalar.activation(vs_row[:], vs_pool[:].indirect(k_list[:, g * PAGE // 16:(g + 1) * PAGE // 16]), ACT.Copy)
             cols = shared.tile([P, PACK], F32, name="vs_cols%d" % g, align_bytes=64, offset=COLS_AT + 64 * g)
-            nc.scalar.dma_start(cols[:], vs_row[0:1, :].rearrange("o (s t) -> o s t", t=PACK))
-            return cols
+            nc.sync.dma_start(cols[:], vs_row[VS_ROW:VS_ROW + 1, :].rearrange("o (s t) -> o s t", t=PACK))
+            vs_cols.append(cols)
 
-        q_codes = sb.tile([P, PASSES * NQ], U32, name="q_codes", align_bytes=64)
-        q_scale = sb.tile([P, PASSES * NQ], U8, name="q_scale", align_bytes=64)
-        words = []
-        for g in range(PAGES):
-            if g == PAGES - 1:
-                nc.vector.quantize_mx(out=q_codes[:].bitcast(FP8X4), scales=q_scale[:],
-                                      in_=q_bf[:].rearrange("p o w j -> p (o w j)"))
-            parted = shared.tile([P, PASSES, PAGE], U16, name="k_words%d" % g, align_bytes=64, offset=WORDS_AT + 4 * PAGE * g)
-            nc.vector.tensor_copy(parted[:], pairs[g][:].bitcast(U16).rearrange("p (n o) -> p o n", o=PASSES))
-            words.append(parted)
-        scores = []
-        for g in range(PAGES):
-            score = ps.tile([P, PAGE], F32, name="score%d" % g)
+        q_codes = [sb.tile([P, NQ], U32, name="q_codes%d" % o, align_bytes=64) for o in range(PASSES)]
+        q_scale = [sb.tile([P, NQ], U8, name="q_scale%d" % o, align_bytes=64) for o in range(PASSES)]
+        pairs = [shared.tile([P, CHUNK], U32, name="k_pairs%d" % c, align_bytes=64, offset=PAIRS_AT[c]) for c in range(CHUNKS)]
+        words = [shared.tile([P, PASSES, CHUNK], U16, name="k_words%d" % c, align_bytes=64, offset=WORDS_AT[c]) for c in range(CHUNKS)]
+        first_page = ps.tile([P, PAGE], F32, name="score_first")
+        scores = [first_page[:, :CHUNK], first_page[:, CHUNK:]]
+        for c in range(2, CHUNKS):
+            bank = ps.tile([P, CHUNK], F32, name="score%d" % c)
+            scores.append(bank[:])
+
+        def gather(c):
+            nc.vector.tensor_copy(pairs[c][:], k_pool[:].bitcast(U32).indirect(k_list[:, c * CHUNK // 16:(c + 1) * CHUNK // 16]))
+
+        def quantize_q(o):
+            nc.vector.quantize_mx(out=q_codes[o][:].bitcast(FP8X4), scales=q_scale[o][:],
+                                  in_=q_bf[o][:].rearrange("p w j -> p (w j)"))
+
+        def part(c):
+            nc.vector.tensor_copy(words[c][:], pairs[c][:].bitcast(U16).rearrange("p (n o) -> p o n", o=PASSES))
+
+        def score(c):
             for o in range(PASSES):
                 nc.tensor.matmul_mx(
-                    out=score[:],
-                    lhsT=q_codes[:, o * NQ:(o + 1) * NQ].bitcast(FP8X4),
-                    lhsT_scale=q_scale[:, o * NQ:(o + 1) * NQ],
-                    rhs=words[g][:, o, :].bitcast(FP4X4),
-                    rhs_scale=k_planes[:, o * N + g * PAGE:o * N + (g + 1) * PAGE],
+                    out=scores[c], lhsT=q_codes[o][:].bitcast(FP8X4), lhsT_scale=q_scale[o][:],
+                    rhs=words[c][:, o, :].bitcast(FP4X4),
+                    rhs_scale=k_planes[:, o * N + c * CHUNK:o * N + (c + 1) * CHUNK],
                     start=(o == 0), stop=(o == PASSES - 1))
-            scores.append(score)
+
+        gather(0)
+        gather(1)
+        part(0)
+        quantize_q(0)
+        gather(2)
+        quantize_q(1)
+        part(1)
+        gather(3)
+        part(2)
+        part(3)
+        for c in range(CHUNKS):
+            score(c)
 
         neg = [sb.tile([P, PACK, P], F32, name="neg_scores%d" % g, align_bytes=64) for g in range(PAGES)]
-        neg_maxes = [shared.tile([P, 1], F32, name="neg_max0", align_bytes=64, offset=V_CODES_AT),
-                     sb.tile([P, 1], F32, name="neg_max1")]
-        vs_cols = [token_scales(g, shared.tile([P, PAGE], F32, name="vs_row%d" % g, align_bytes=64, offset=ROWS_AT + 4 * PAGE * g))
-                   for g in range(PAGES)]
-        for g in range(PAGES):
-            nc.vector.tensor_scalar(neg[g][:], scores[g][:].rearrange("q (s t) -> q t s", t=PACK), -1.0,
-                                    neg_maxes[g - 1][:] if g else None,
-                                    op0=ALU.mult, op1=ALU.min, accum_out=neg_maxes[g][:])
-        neg_max = neg_maxes[-1]
+        half = CHUNK // PACK
+        stretches = [(first_page[:], neg[0][:]), (scores[2], neg[1][:, :, :half]), (scores[3], neg[1][:, :, half:])]
+        neg_max = None
+        for i, (src, dst) in enumerate(stretches):
+            so_far = sb.tile([P, 1], F32, name="neg_max%d" % i)
+            nc.vector.tensor_scalar(dst, src.rearrange("q (s t) -> q t s", t=PACK), -1.0,
+                                    neg_max[:] if i else None, op0=ALU.mult, op1=ALU.min, accum_out=so_far[:])
+            neg_max = so_far
 
-        ident = shared.tile([P, P], F32, name="ident", align_bytes=64, offset=VS_AT)
+        ident = shared.tile([P, P], F32, name="ident", align_bytes=64, offset=IDENT_AT)
         make_identity(nc, ident[:])
 
         v_codes = shared.tile([P, PAGES * DV], U32, name="v_codes", align_bytes=64, offset=V_CODES_AT)
         nc.vector.tensor_copy(v_codes[:], v_pool[:].bitcast(U32).indirect(v_list[:]))
 
-        prob = sb.tile([P, N], F32, name="prob", align_bytes=64)
+        prob = shared.tile([P, N], F32, name="prob", align_bytes=64, offset=VS_AT)
         for g in range(PAGES):
             for t in range(PACK):
                 c0 = g * PAGE + t * P
@@ -172,7 +184,7 @@ def tile_attend_pkv4_soft_kernel(tc, qT, k_words, k_scales, v_words, v_scales, v
             for t in range(PACK):
                 c0 = g * PAGE + t * P
                 nc.tensor.transpose(turned[:, t, :], prob[:, c0:c0 + P], ident[:])
-            w = shared.tile([P, NQ, PACK], BF16, name="w_bf%d" % g, align_bytes=64, offset=V_AT + 2 * PAGE * g)
+            w = sb.tile([P, NQ, PACK], BF16, name="w_bf%d" % g, align_bytes=64)
             nc.vector.tensor_tensor(w[:], turned[:].rearrange("s t q -> s q t"),
                                     vs_cols[g][:].unsqueeze(1).to_broadcast([P, NQ, PACK]), ALU.mult)
             w_bf.append(w)

@@ -29,15 +29,14 @@ K_FIRST = 768
 VS_WIDE = 32
 VS_FILLED = 2816
 VS_ROW = 8
-CHUNK = 256
-CHUNKS = N // CHUNK
 
 KB = 1024
-PAIRS_AT = (0, KB, 3 * KB, 6 * KB)
-WORDS_AT = (2 * KB, 5 * KB, 7 * KB, 8 * KB)
-Q_RAW_AT = (3 * KB, 5 * KB + KB // 2)
-IDENT_AT = WORDS_AT[2] + KB // 2
-V_CODES_AT = WORDS_AT[3]
+PAIRS_AT = (0, 2 * KB)
+WORDS_AT = (4 * KB, 6 * KB)
+Q_RAW_AT = (8 * KB, WORDS_AT[1])
+IDENT_AT = WORDS_AT[0]
+V_CODES_AT = 10 * KB
+MAX_AT = (V_CODES_AT, 0)
 COLS_AT = V_CODES_AT + 4 * PAGES * DV
 VS_AT = COLS_AT + 64 * PAGES
 
@@ -84,9 +83,9 @@ def tile_attend_pkv4_soft_kernel(tc, qT, k_words, k_scales, v_words, v_scales, v
         nc.scalar.activation(vs_pool[:, :VS_FILLED].rearrange("p (a c) -> p a c", c=VS_WIDE),
                              vs_head[:].unsqueeze(1).to_broadcast([P, VS_FILLED // VS_WIDE, VS_WIDE]), ACT.Copy)
 
-        q_bf = [sb.tile([P, NQ, PACK], BF16, name="q_bf%d" % o, align_bytes=64) for o in range(PASSES)]
+        q_bf = sb.tile([P, PASSES, NQ, PACK], BF16, name="q_bf", align_bytes=64)
         for o in range(PASSES):
-            nc.scalar.copy(q_bf[o][:], q_raw[o][:].rearrange("p j w -> p w j"))
+            nc.scalar.copy(q_bf[:, o], q_raw[o][:].rearrange("p j w -> p w j"))
 
         k_scale_rows = sb.tile([P, N], U8, name="k_scale_rows", align_bytes=64)
         nc.vector.tensor_copy(k_scale_rows[:], k_scale_pool[:].indirect(k_list[:]))
@@ -111,55 +110,40 @@ def tile_attend_pkv4_soft_kernel(tc, qT, k_words, k_scales, v_words, v_scales, v
             nc.sync.dma_start(cols[:], vs_row[VS_ROW:VS_ROW + 1, :].rearrange("o (s t) -> o s t", t=PACK))
             vs_cols.append(cols)
 
-        q_codes = [sb.tile([P, NQ], U32, name="q_codes%d" % o, align_bytes=64) for o in range(PASSES)]
-        q_scale = [sb.tile([P, NQ], U8, name="q_scale%d" % o, align_bytes=64) for o in range(PASSES)]
-        pairs = [shared.tile([P, CHUNK], U32, name="k_pairs%d" % c, align_bytes=64, offset=PAIRS_AT[c]) for c in range(CHUNKS)]
-        words = [shared.tile([P, PASSES, CHUNK], U16, name="k_words%d" % c, align_bytes=64, offset=WORDS_AT[c]) for c in range(CHUNKS)]
-        first_page = ps.tile([P, PAGE], F32, name="score_first")
-        scores = [first_page[:, :CHUNK], first_page[:, CHUNK:]]
-        for c in range(2, CHUNKS):
-            bank = ps.tile([P, CHUNK], F32, name="score%d" % c)
-            scores.append(bank[:])
-
-        def gather(c):
-            nc.vector.tensor_copy(pairs[c][:], k_pool[:].bitcast(U32).indirect(k_list[:, c * CHUNK // 16:(c + 1) * CHUNK // 16]))
-
-        def quantize_q(o):
-            nc.vector.quantize_mx(out=q_codes[o][:].bitcast(FP8X4), scales=q_scale[o][:],
-                                  in_=q_bf[o][:].rearrange("p w j -> p (w j)"))
-
-        def part(c):
-            nc.vector.tensor_copy(words[c][:], pairs[c][:].bitcast(U16).rearrange("p (n o) -> p o n", o=PASSES))
-
-        def score(c):
+        pairs = []
+        for g in range(PAGES):
+            both = shared.tile([P, PAGE], U32, name="k_pairs%d" % g, align_bytes=64, offset=PAIRS_AT[g])
+            nc.vector.tensor_copy(both[:], k_pool[:].bitcast(U32).indirect(k_list[:, g * PAGE // 16:(g + 1) * PAGE // 16]))
+            pairs.append(both)
+        q_codes = sb.tile([P, PASSES * NQ], U32, name="q_codes", align_bytes=64)
+        q_scale = sb.tile([P, PASSES * NQ], U8, name="q_scale", align_bytes=64)
+        words = []
+        for g in range(PAGES):
+            if g == PAGES - 1:
+                nc.vector.quantize_mx(out=q_codes[:].bitcast(FP8X4), scales=q_scale[:],
+                                      in_=q_bf[:].rearrange("p o w j -> p (o w j)"))
+            parted = shared.tile([P, PASSES, PAGE], U16, name="k_words%d" % g, align_bytes=64, offset=WORDS_AT[g])
+            nc.vector.tensor_copy(parted[:], pairs[g][:].bitcast(U16).rearrange("p (n o) -> p o n", o=PASSES))
+            words.append(parted)
+        scores = []
+        for g in range(PAGES):
+            score = ps.tile([P, PAGE], F32, name="score%d" % g)
             for o in range(PASSES):
                 nc.tensor.matmul_mx(
-                    out=scores[c], lhsT=q_codes[o][:].bitcast(FP8X4), lhsT_scale=q_scale[o][:],
-                    rhs=words[c][:, o, :].bitcast(FP4X4),
-                    rhs_scale=k_planes[:, o * N + c * CHUNK:o * N + (c + 1) * CHUNK],
+                    out=score[:],
+                    lhsT=q_codes[:, o * NQ:(o + 1) * NQ].bitcast(FP8X4),
+                    lhsT_scale=q_scale[:, o * NQ:(o + 1) * NQ],
+                    rhs=words[g][:, o, :].bitcast(FP4X4),
+                    rhs_scale=k_planes[:, o * N + g * PAGE:o * N + (g + 1) * PAGE],
                     start=(o == 0), stop=(o == PASSES - 1))
-
-        gather(0)
-        gather(1)
-        part(0)
-        quantize_q(0)
-        gather(2)
-        quantize_q(1)
-        part(1)
-        gather(3)
-        part(2)
-        part(3)
-        for c in range(CHUNKS):
-            score(c)
+            scores.append(score)
 
         neg = [sb.tile([P, PACK, P], F32, name="neg_scores%d" % g, align_bytes=64) for g in range(PAGES)]
-        half = CHUNK // PACK
-        stretches = [(first_page[:], neg[0][:]), (scores[2], neg[1][:, :, :half]), (scores[3], neg[1][:, :, half:])]
         neg_max = None
-        for i, (src, dst) in enumerate(stretches):
-            so_far = sb.tile([P, 1], F32, name="neg_max%d" % i)
-            nc.vector.tensor_scalar(dst, src.rearrange("q (s t) -> q t s", t=PACK), -1.0,
-                                    neg_max[:] if i else None, op0=ALU.mult, op1=ALU.min, accum_out=so_far[:])
+        for g in range(PAGES):
+            so_far = shared.tile([P, 1], F32, name="neg_max%d" % g, align_bytes=64, offset=MAX_AT[g])
+            nc.vector.tensor_scalar(neg[g][:], scores[g][:].rearrange("q (s t) -> q t s", t=PACK), -1.0,
+                                    neg_max[:] if g else None, op0=ALU.mult, op1=ALU.min, accum_out=so_far[:])
             neg_max = so_far
 
         ident = shared.tile([P, P], F32, name="ident", align_bytes=64, offset=IDENT_AT)

@@ -32,9 +32,9 @@ VS_ROW = 8
 
 KB = 1024
 PAIRS_AT = (0, 2 * KB)
-WORDS_AT = (4 * KB, 6 * KB)
-Q_RAW_AT = (8 * KB, WORDS_AT[1])
-IDENT_AT = WORDS_AT[0]
+Q_RAW_AT = (6 * KB, 8 * KB)
+WORDS_AT = ((4 * KB, Q_RAW_AT[0]), (Q_RAW_AT[1], Q_RAW_AT[1] + KB))
+IDENT_AT = WORDS_AT[0][1]
 V_CODES_AT = 10 * KB
 MAX_AT = (V_CODES_AT, 0)
 COLS_AT = V_CODES_AT + 4 * PAGES * DV
@@ -83,9 +83,9 @@ def tile_attend_pkv4_soft_kernel(tc, qT, k_words, k_scales, v_words, v_scales, v
         nc.scalar.activation(vs_pool[:, :VS_FILLED].rearrange("p (a c) -> p a c", c=VS_WIDE),
                              vs_head[:].unsqueeze(1).to_broadcast([P, VS_FILLED // VS_WIDE, VS_WIDE]), ACT.Copy)
 
-        q_bf = sb.tile([P, PASSES, NQ, PACK], BF16, name="q_bf", align_bytes=64)
+        q_bf = [sb.tile([P, NQ, PACK], BF16, name="q_bf%d" % o, align_bytes=64) for o in range(PASSES)]
         for o in range(PASSES):
-            nc.scalar.copy(q_bf[:, o], q_raw[o][:].rearrange("p j w -> p w j"))
+            nc.scalar.copy(q_bf[o][:], q_raw[o][:].rearrange("p j w -> p w j"))
 
         k_scale_rows = sb.tile([P, N], U8, name="k_scale_rows", align_bytes=64)
         nc.vector.tensor_copy(k_scale_rows[:], k_scale_pool[:].indirect(k_list[:]))
@@ -115,25 +115,20 @@ def tile_attend_pkv4_soft_kernel(tc, qT, k_words, k_scales, v_words, v_scales, v
             both = shared.tile([P, PAGE], U32, name="k_pairs%d" % g, align_bytes=64, offset=PAIRS_AT[g])
             nc.vector.tensor_copy(both[:], k_pool[:].bitcast(U32).indirect(k_list[:, g * PAGE // 16:(g + 1) * PAGE // 16]))
             pairs.append(both)
-        q_codes = sb.tile([P, PASSES * NQ], U32, name="q_codes", align_bytes=64)
-        q_scale = sb.tile([P, PASSES * NQ], U8, name="q_scale", align_bytes=64)
-        words = []
-        for g in range(PAGES):
-            if g == PAGES - 1:
-                nc.vector.quantize_mx(out=q_codes[:].bitcast(FP8X4), scales=q_scale[:],
-                                      in_=q_bf[:].rearrange("p o w j -> p (o w j)"))
-            parted = shared.tile([P, PASSES, PAGE], U16, name="k_words%d" % g, align_bytes=64, offset=WORDS_AT[g])
-            nc.vector.tensor_copy(parted[:], pairs[g][:].bitcast(U16).rearrange("p (n o) -> p o n", o=PASSES))
-            words.append(parted)
+        q_codes = [sb.tile([P, NQ], U32, name="q_codes%d" % o, align_bytes=64) for o in range(PASSES)]
+        q_scale = [sb.tile([P, NQ], U8, name="q_scale%d" % o, align_bytes=64) for o in range(PASSES)]
         scores = []
         for g in range(PAGES):
             score = ps.tile([P, PAGE], F32, name="score%d" % g)
             for o in range(PASSES):
+                words = shared.tile([P, PAGE], U16, name="k_words%d_%d" % (g, o), align_bytes=64, offset=WORDS_AT[g][o])
+                nc.vector.tensor_copy(words[:], pairs[g][:].bitcast(U16).rearrange("p (n o) -> p o n", o=PASSES)[:, o, :])
+                if g == 0:
+                    nc.vector.quantize_mx(out=q_codes[o][:].bitcast(FP8X4), scales=q_scale[o][:],
+                                          in_=q_bf[o][:].rearrange("p w j -> p (w j)"))
                 nc.tensor.matmul_mx(
-                    out=score[:],
-                    lhsT=q_codes[:, o * NQ:(o + 1) * NQ].bitcast(FP8X4),
-                    lhsT_scale=q_scale[:, o * NQ:(o + 1) * NQ],
-                    rhs=words[g][:, o, :].bitcast(FP4X4),
+                    out=score[:], lhsT=q_codes[o][:].bitcast(FP8X4), lhsT_scale=q_scale[o][:],
+                    rhs=words[:].bitcast(FP4X4),
                     rhs_scale=k_planes[:, o * N + g * PAGE:o * N + (g + 1) * PAGE],
                     start=(o == 0), stop=(o == PASSES - 1))
             scores.append(score)

@@ -11,6 +11,7 @@ PAGES = N // PAGE
 POOL_PAGES = T // PAGE
 PASSES = D // PAGE
 QUADS = 4
+HALF = PAGE // 2
 
 FLOPS = 2 * NQ * N * (D + DV)
 BYTES = 4 * D * NQ + 4 * P * T + PASSES * 16 * T + 4 * P * POOL_PAGES * DV + POOL_PAGES * 16 * DV + 4 * T + 2 * P * (N + PAGES * DV) // 16 + 4 * NQ * DV
@@ -31,13 +32,15 @@ VS_FILLED = 2816
 VS_ROW = 8
 
 KB = 1024
-PAIRS_AT = (0, 2 * KB)
+K_SCALES_AT = 0
+V_SCALES_AT = 4 * KB
 Q_RAW_AT = (6 * KB, 8 * KB)
-WORDS_AT = ((4 * KB, Q_RAW_AT[0]), (Q_RAW_AT[1], Q_RAW_AT[1] + KB))
-IDENT_AT = WORDS_AT[0][1]
-V_CODES_AT = 10 * KB
-MAX_AT = (V_CODES_AT, 0)
-COLS_AT = V_CODES_AT + 4 * PAGES * DV
+Q_BF_AT = (10 * KB, 11 * KB)
+PAIRS_AT = (12 * KB, 14 * KB, Q_BF_AT[1])
+WORDS_AT = (15 * KB, Q_RAW_AT[0], Q_RAW_AT[1], Q_RAW_AT[1] + KB)
+V_CODES_AT = Q_RAW_AT[1]
+MAX_AT = (PAIRS_AT[0] + 64, PAIRS_AT[0] + 128, PAIRS_AT[0])
+COLS_AT = 16 * KB
 VS_AT = COLS_AT + 64 * PAGES
 
 
@@ -52,19 +55,18 @@ def tile_attend_pkv4_soft_kernel(tc, qT, k_words, k_scales, v_words, v_scales, v
         k_list = lists.tile([P, N // 16], U16, name="k_list")
         v_list = lists.tile([P, PAGES * DV // 16], U16, name="v_list")
 
-        k_scale_pool = sb.tile([P, T], U8, name="k_scale_pool", align_bytes=64)
-        v_scale_pool = sb.tile([P, POOL_PAGES * DV], U8, name="v_scale_pool", align_bytes=64)
+        k_scale_pool = shared.tile([P, T], U8, name="k_scale_pool", align_bytes=64, offset=K_SCALES_AT)
+        v_scale_pool = shared.tile([P, POOL_PAGES * DV], U8, name="v_scale_pool", align_bytes=64, offset=V_SCALES_AT)
         vs_pool = shared.tile([P, T], F32, name="vs_pool", align_bytes=64, offset=VS_AT)
         k_pool = sb.tile([P, T], I32, name="k_pool", align_bytes=64)
         q_raw = [shared.tile([P, PACK, NQ], F32, name="q_raw%d" % o, align_bytes=64, offset=Q_RAW_AT[o]) for o in range(PASSES)]
-        k_planes = sb.tile([P, PASSES * N], U8, name="k_planes", align_bytes=64)
-        v_plane = sb.tile([P, PAGES * DV], U8, name="v_plane", align_bytes=64)
+        ident = sb.tile([P, P], F32, name="ident", align_bytes=64)
 
         nc.vector.memset(k_scale_pool[:].bitcast(I32), 0)
         nc.vector.memset(v_scale_pool[:].bitcast(I32), 0)
-        nc.vector.memset(k_planes[:].bitcast(I32), 0)
-        nc.vector.memset(v_plane[:].bitcast(I32), 0)
         nc.vector.memset(vs_pool[:, VS_FILLED:].bitcast(I32), 0)
+        nc.vector.memset(ident[:], 0.0)
+        make_identity(nc, ident[:], nomemset=True)
 
         k_rows = k_words[0].rearrange("g t b -> g (t b)").bitcast(I32)
         nc.sync.dma_start(k_pool[:, :K_FIRST], k_rows[:, :K_FIRST])
@@ -83,12 +85,13 @@ def tile_attend_pkv4_soft_kernel(tc, qT, k_words, k_scales, v_words, v_scales, v
         nc.scalar.activation(vs_pool[:, :VS_FILLED].rearrange("p (a c) -> p a c", c=VS_WIDE),
                              vs_head[:].unsqueeze(1).to_broadcast([P, VS_FILLED // VS_WIDE, VS_WIDE]), ACT.Copy)
 
-        q_bf = [sb.tile([P, NQ, PACK], BF16, name="q_bf%d" % o, align_bytes=64) for o in range(PASSES)]
+        q_bf = [shared.tile([P, NQ, PACK], BF16, name="q_bf%d" % o, align_bytes=64, offset=Q_BF_AT[o]) for o in range(PASSES)]
         for o in range(PASSES):
-            nc.scalar.copy(q_bf[o][:], q_raw[o][:].rearrange("p j w -> p w j"))
+            nc.scalar.activation(q_bf[o][:], q_raw[o][:].rearrange("p j w -> p w j"), ACT.Copy, scale=-1.0)
 
         k_scale_rows = sb.tile([P, N], U8, name="k_scale_rows", align_bytes=64)
         nc.vector.tensor_copy(k_scale_rows[:], k_scale_pool[:].indirect(k_list[:]))
+        k_planes = shared.tile([P, PASSES * N], U8, name="k_planes", align_bytes=64, offset=K_SCALES_AT)
         for a in (0, 2, 1, 3):
             nc.sync.dma_start(k_planes[:].bitcast(I32)[32 * a:32 * a + 4, :].rearrange("r (o c) -> r o c", o=PASSES),
                               k_scale_rows[:].bitcast(I32)[32 * a:32 * (a + 1):4, :])
@@ -98,6 +101,7 @@ def tile_attend_pkv4_soft_kernel(tc, qT, k_words, k_scales, v_words, v_scales, v
                           v_words.rearrange("u g e r -> g u (e r)").bitcast(I32))
         v_scale_rows = sb.tile([P, PAGES * DV], U8, name="v_scale_rows", align_bytes=64)
         nc.vector.tensor_copy(v_scale_rows[:], v_scale_pool[:].indirect(v_list[:]))
+        v_plane = shared.tile([P, PAGES * DV], U8, name="v_plane", align_bytes=64, offset=V_SCALES_AT)
         for a in range(QUADS):
             nc.sync.dma_start(v_plane[:].bitcast(I32)[32 * a:32 * a + 4, :],
                               v_scale_rows[:].bitcast(I32)[32 * a:32 * (a + 1):8, :])
@@ -110,48 +114,63 @@ def tile_attend_pkv4_soft_kernel(tc, qT, k_words, k_scales, v_words, v_scales, v
             nc.sync.dma_start(cols[:], vs_row[VS_ROW:VS_ROW + 1, :].rearrange("o (s t) -> o s t", t=PACK))
             vs_cols.append(cols)
 
-        pairs = []
-        for g in range(PAGES):
-            both = shared.tile([P, PAGE], U32, name="k_pairs%d" % g, align_bytes=64, offset=PAIRS_AT[g])
-            nc.vector.tensor_copy(both[:], k_pool[:].bitcast(U32).indirect(k_list[:, g * PAGE // 16:(g + 1) * PAGE // 16]))
-            pairs.append(both)
+        chunks = ((0, PAGE), (PAGE, HALF), (PAGE + HALF, HALF))
+        pairs = [None] * len(chunks)
+        scores = [ps.tile([P, width], F32, name="score%d" % c) for c, (first, width) in enumerate(chunks)]
         q_codes = [sb.tile([P, NQ], U32, name="q_codes%d" % o, align_bytes=64) for o in range(PASSES)]
         q_scale = [sb.tile([P, NQ], U8, name="q_scale%d" % o, align_bytes=64) for o in range(PASSES)]
-        scores = []
-        for g in range(PAGES):
-            score = ps.tile([P, PAGE], F32, name="score%d" % g)
-            for o in range(PASSES):
-                words = shared.tile([P, PAGE], U16, name="k_words%d_%d" % (g, o), align_bytes=64, offset=WORDS_AT[g][o])
-                nc.vector.tensor_copy(words[:], pairs[g][:].bitcast(U16).rearrange("p (n o) -> p o n", o=PASSES)[:, o, :])
-                if g == 0:
-                    nc.vector.quantize_mx(out=q_codes[o][:].bitcast(FP8X4), scales=q_scale[o][:],
-                                          in_=q_bf[o][:].rearrange("p w j -> p (w j)"))
-                nc.tensor.matmul_mx(
-                    out=score[:], lhsT=q_codes[o][:].bitcast(FP8X4), lhsT_scale=q_scale[o][:],
-                    rhs=words[:].bitcast(FP4X4),
-                    rhs_scale=k_planes[:, o * N + g * PAGE:o * N + (g + 1) * PAGE],
-                    start=(o == 0), stop=(o == PASSES - 1))
-            scores.append(score)
 
-        neg = [sb.tile([P, PACK, P], F32, name="neg_scores%d" % g, align_bytes=64) for g in range(PAGES)]
-        neg_max = None
-        for g in range(PAGES):
-            so_far = shared.tile([P, 1], F32, name="neg_max%d" % g, align_bytes=64, offset=MAX_AT[g])
-            nc.vector.tensor_scalar(neg[g][:], scores[g][:].rearrange("q (s t) -> q t s", t=PACK), -1.0,
-                                    neg_max[:] if g else None, op0=ALU.mult, op1=ALU.min, accum_out=so_far[:])
-            neg_max = so_far
+        def gather_keys(c):
+            first, width = chunks[c]
+            both = shared.tile([P, width], U32, name="k_pairs%d" % c, align_bytes=64, offset=PAIRS_AT[c])
+            nc.vector.tensor_copy(both[:], k_pool[:].bitcast(U32).indirect(k_list[:, first // 16:(first + width) // 16]))
+            pairs[c] = both[:].bitcast(U16).rearrange("p (n o) -> p o n", o=PASSES)
 
-        ident = shared.tile([P, P], F32, name="ident", align_bytes=64, offset=IDENT_AT)
-        make_identity(nc, ident[:])
+        def score_pass(c, o, words):
+            first, width = chunks[c]
+            nc.tensor.matmul_mx(
+                out=scores[c][:], lhsT=q_codes[o][:].bitcast(FP8X4), lhsT_scale=q_scale[o][:],
+                rhs=words.bitcast(FP4X4),
+                rhs_scale=k_planes[:, o * N + first:o * N + first + width],
+                start=(o == 0), stop=(o == PASSES - 1))
+
+        gather_keys(0)
+        gather_keys(1)
+        for o in range(PASSES):
+            words = shared.tile([P, PAGE], U16, name="k_words0_%d" % o, align_bytes=64, offset=WORDS_AT[o])
+            nc.vector.tensor_copy(words[:], pairs[0][:, o, :])
+            nc.vector.quantize_mx(out=q_codes[o][:].bitcast(FP8X4), scales=q_scale[o][:],
+                                  in_=q_bf[o][:].rearrange("p w j -> p (w j)"))
+            score_pass(0, o, words[:])
+        gather_keys(2)
+        words = shared.tile([P, PASSES, HALF], U16, name="k_words1", align_bytes=64, offset=WORDS_AT[2])
+        nc.vector.tensor_copy(words[:], pairs[1])
+        for o in range(PASSES):
+            score_pass(1, o, words[:, o, :])
+        for o in range(PASSES):
+            words = shared.tile([P, HALF], U16, name="k_words2_%d" % o, align_bytes=64, offset=WORDS_AT[3] + 2 * HALF * o)
+            nc.vector.tensor_copy(words[:], pairs[2][:, o, :])
+            score_pass(2, o, words[:])
+
+        neg = [sb.tile([P, PACK, width // PACK], F32, name="neg_scores%d" % c, align_bytes=64) for c, (first, width) in enumerate(chunks)]
+        least = [shared.tile([P, 1], F32, name="least%d" % c, align_bytes=64, offset=MAX_AT[c]) for c in range(len(chunks))]
+        for c in range(2):
+            nc.vector.tensor_scalar(neg[c][:], scores[c][:].rearrange("q (s t) -> q t s", t=PACK), 1.0, None,
+                                    op0=ALU.mult, op1=ALU.min, accum_out=least[c][:])
+        nc.vector.tensor_scalar(neg[2][:].rearrange("q t s -> q (t s)"), scores[2][:], least[0][:], least[1][:],
+                                op0=ALU.min, op1=ALU.min, accum_out=least[2][:])
+        neg_max = least[2]
 
         v_codes = shared.tile([P, PAGES * DV], U32, name="v_codes", align_bytes=64, offset=V_CODES_AT)
         nc.vector.tensor_copy(v_codes[:], v_pool[:].bitcast(U32).indirect(v_list[:]))
 
         prob = shared.tile([P, N], F32, name="prob", align_bytes=64, offset=VS_AT)
-        for g in range(PAGES):
-            for t in range(PACK):
-                c0 = g * PAGE + t * P
-                nc.scalar.activation(prob[:, c0:c0 + P], neg[g][:, t, :], ACT.Exp, bias=neg_max[:], scale=-1.0)
+        dealt = prob[:].rearrange("q (g t s) -> q g t s", g=PAGES, t=PACK)
+        for t in range(PACK):
+            nc.scalar.activation(dealt[:, 0, t, :], neg[0][:, t, :], ACT.Exp, bias=neg_max[:], scale=-1.0)
+        nc.scalar.activation(dealt[:, 1, :, P // 2:], scores[2][:].rearrange("q (s t) -> q t s", t=PACK), ACT.Exp, bias=neg_max[:], scale=-1.0)
+        for t in range(PACK):
+            nc.scalar.activation(dealt[:, 1, t, :P // 2], neg[1][:, t, :], ACT.Exp, bias=neg_max[:], scale=-1.0)
         prob_again = sb.tile([P, N], F32, name="prob_again", align_bytes=64)
         total = sb.tile([P, 1], F32, name="total")
         nc.scalar.activation(prob_again[:], prob[:], ACT.Copy, accum_out=total[:])

@@ -86,15 +86,16 @@ def tile_attend_pkv4_soft_kernel(tc, qT, k_words, k_scales, v_words, v_scales, v
                              vs_head[:].unsqueeze(1).to_broadcast([P, VS_FILLED // VS_WIDE, VS_WIDE]), ACT.Copy)
 
         q_bf = [shared.tile([P, NQ, PACK], BF16, name="q_bf%d" % o, align_bytes=64, offset=Q_BF_AT[o]) for o in range(PASSES)]
-        for o in range(PASSES):
-            nc.scalar.activation(q_bf[o][:], q_raw[o][:].rearrange("p j w -> p w j"), ACT.Copy, scale=-1.0)
 
         k_scale_rows = sb.tile([P, N], U8, name="k_scale_rows", align_bytes=64)
         nc.vector.tensor_copy(k_scale_rows[:], k_scale_pool[:].indirect(k_list[:]))
         k_planes = shared.tile([P, PASSES * N], U8, name="k_planes", align_bytes=64, offset=K_SCALES_AT)
         for a in (0, 2, 1, 3):
-            nc.sync.dma_start(k_planes[:].bitcast(I32)[32 * a:32 * a + 4, :].rearrange("r (o c) -> r o c", o=PASSES),
-                              k_scale_rows[:].bitcast(I32)[32 * a:32 * (a + 1):4, :])
+            queue = nc.sync if a < 2 else nc.scalar
+            queue.dma_start(k_planes[:].bitcast(I32)[32 * a:32 * a + 4, :].rearrange("r (o c) -> r o c", o=PASSES),
+                            k_scale_rows[:].bitcast(I32)[32 * a:32 * (a + 1):4, :])
+        for o in range(PASSES):
+            nc.scalar.activation(q_bf[o][:], q_raw[o][:].rearrange("p j w -> p w j"), ACT.Copy, scale=-1.0)
         nc.sync.dma_start(vs_pool[VS_ROW:VS_ROW + 1, :], vs[0:1, :])
         v_pool = sb.tile([P, POOL_PAGES * DV], I32, name="v_pool", align_bytes=64)
         nc.sync.dma_start(v_pool[:].rearrange("g (u e) -> g u e", u=POOL_PAGES),

@@ -36,11 +36,11 @@ K_SCALES_AT = 0
 V_SCALES_AT = 4 * KB
 Q_RAW_AT = (6 * KB, 8 * KB)
 Q_BF_AT = (10 * KB, 11 * KB)
-PAIRS_AT = (12 * KB, 14 * KB, Q_BF_AT[1])
-WORDS_AT = (15 * KB, Q_RAW_AT[0], Q_RAW_AT[1], Q_RAW_AT[1] + KB)
-V_CODES_AT = Q_RAW_AT[1]
+PAIRS_AT = (12 * KB, 14 * KB, Q_RAW_AT[1])
+WORDS_AT = (15 * KB, Q_RAW_AT[0], Q_RAW_AT[1] + KB, 16 * KB)
+V_CODES_AT = WORDS_AT[3]
 MAX_AT = (PAIRS_AT[0] + 64, PAIRS_AT[0] + 128, PAIRS_AT[0])
-COLS_AT = 16 * KB
+COLS_AT = V_CODES_AT + 4 * PAGES * DV
 VS_AT = COLS_AT + 64 * PAGES
 
 
@@ -95,7 +95,8 @@ def tile_attend_pkv4_soft_kernel(tc, qT, k_words, k_scales, v_words, v_scales, v
             queue.dma_start(k_planes[:].bitcast(I32)[32 * a:32 * a + 4, :].rearrange("r (o c) -> r o c", o=PASSES),
                             k_scale_rows[:].bitcast(I32)[32 * a:32 * (a + 1):4, :])
         for o in range(PASSES):
-            nc.scalar.activation(q_bf[o][:], q_raw[o][:].rearrange("p j w -> p w j"), ACT.Copy, scale=-1.0)
+            nc.scalar.activation(q_bf[o][:].rearrange("p (c i) j -> p c j i", i=PACK),
+                                 q_raw[o][:].rearrange("p j (c i) -> p c j i", i=PACK), ACT.Copy, scale=-1.0)
         nc.sync.dma_start(vs_pool[VS_ROW:VS_ROW + 1, :], vs[0:1, :])
         v_pool = sb.tile([P, POOL_PAGES * DV], I32, name="v_pool", align_bytes=64)
         nc.sync.dma_start(v_pool[:].rearrange("g (u e) -> g u e", u=POOL_PAGES),

@@ -113,7 +113,7 @@ def tile_attend_pkv4_soft_kernel(tc, qT, k_words, k_scales, v_words, v_scales, v
             vs_row = sb.tile([P, PAGE], F32, name="vs_row%d" % g, align_bytes=64)
             nc.scalar.activation(vs_row[:], vs_pool[:].indirect(k_list[:, g * PAGE // 16:(g + 1) * PAGE // 16]), ACT.Copy)
             cols = shared.tile([P, PACK], F32, name="vs_cols%d" % g, align_bytes=64, offset=COLS_AT + 64 * g)
-            nc.sync.dma_start(cols[:], vs_row[VS_ROW:VS_ROW + 1, :].rearrange("o (s t) -> o s t", t=PACK))
+            nc.scalar.dma_start(cols[:], vs_row[VS_ROW:VS_ROW + 1, :].rearrange("o (s t) -> o s t", t=PACK))
             vs_cols.append(cols)
 
         chunks = ((0, PAGE), (PAGE, HALF), (PAGE + HALF, HALF))

@@ -28,7 +28,7 @@ ALU = mybir.AluOpType
 ACT = mybir.ActivationFunctionType
 K_FIRST = 768
 VS_WIDE = 32
-VS_FILLED = 2816
+VS_FILLED = 3392
 VS_ROW = 8
 
 KB = 1024
@@ -170,9 +170,10 @@ def tile_attend_pkv4_soft_kernel(tc, qT, k_words, k_scales, v_words, v_scales, v
         dealt = prob[:].rearrange("q (g t s) -> q g t s", g=PAGES, t=PACK)
         for t in range(PACK):
             nc.scalar.activation(dealt[:, 0, t, :], neg[0][:, t, :], ACT.Exp, bias=neg_max[:], scale=-1.0)
-        nc.scalar.activation(dealt[:, 1, :, P // 2:], scores[2][:].rearrange("q (s t) -> q t s", t=PACK), ACT.Exp, bias=neg_max[:], scale=-1.0)
-        for t in range(PACK):
-            nc.scalar.activation(dealt[:, 1, t, :P // 2], neg[1][:, t, :], ACT.Exp, bias=neg_max[:], scale=-1.0)
+        last = scores[2][:].rearrange("q (s t) -> q t s", t=PACK)
+        for t in range(0, PACK, 2):
+            nc.scalar.activation(dealt[:, 1, t:t + 2, :P // 2], neg[1][:, t:t + 2, :], ACT.Exp, bias=neg_max[:], scale=-1.0)
+            nc.scalar.activation(dealt[:, 1, t:t + 2, P // 2:], last[:, t:t + 2, :], ACT.Exp, bias=neg_max[:], scale=-1.0)
         prob_again = sb.tile([P, N], F32, name="prob_again", align_bytes=64)
         total = sb.tile([P, 1], F32, name="total")
         nc.scalar.activation(prob_again[:], prob[:], ACT.Copy, accum_out=total[:])

@@ -144,11 +144,12 @@ def tile_attend_pkv4_soft_kernel(tc, qT, k_words, k_scales, v_words, v_scales, v
             nc.vector.quantize_mx(out=q_codes[o][:].bitcast(FP8X4), scales=q_scale[o][:],
                                   in_=q_bf[o][:].rearrange("p w j -> p (w j)"))
             score_pass(0, o, words[:])
-        gather_keys(2)
-        words = shared.tile([P, PASSES, HALF], U16, name="k_words1", align_bytes=64, offset=WORDS_AT[2])
-        nc.vector.tensor_copy(words[:], pairs[1])
         for o in range(PASSES):
-            score_pass(1, o, words[:, o, :])
+            words = shared.tile([P, HALF], U16, name="k_words1_%d" % o, align_bytes=64, offset=WORDS_AT[2] + 2 * HALF * o)
+            nc.vector.tensor_copy(words[:], pairs[1][:, o, :])
+            score_pass(1, o, words[:])
+            if o == 0:
+                gather_keys(2)
         for o in range(PASSES):
             words = shared.tile([P, HALF], U16, name="k_words2_%d" % o, align_bytes=64, offset=WORDS_AT[3] + 2 * HALF * o)
             nc.vector.tensor_copy(words[:], pairs[2][:, o, :])

from contextlib import ExitStack

import concourse.mybir as mybir
from concourse.masks import make_identity

N, T, D, DV, NQ = 1024, 4096, 1024, 256, 128
PAGE = 512
P = 128
PACK = 4
PAGES = N // PAGE
POOL_PAGES = T // PAGE
PASSES = D // PAGE
QUADS = 4
HALF = PAGE // 2

FLOPS = 2 * NQ * N * (D + DV)
BYTES = 4 * D * NQ + 4 * P * T + PASSES * 16 * T + 4 * P * POOL_PAGES * DV + POOL_PAGES * 16 * DV + 4 * T + 2 * P * (N + PAGES * DV) // 16 + 4 * NQ * DV

F32 = mybir.dt.float32
BF16 = mybir.dt.bfloat16
I32 = mybir.dt.int32
U32 = mybir.dt.uint32
U16 = mybir.dt.uint16
U8 = mybir.dt.uint8
FP8X4 = mybir.dt.float8_e4m3fn_x4
FP4X4 = mybir.dt.float4_e2m1fn_x4
ALU = mybir.AluOpType
ACT = mybir.ActivationFunctionType
K_FIRST = 768
VS_WIDE = 32
VS_FILLED = 3392
VS_ROW = 8

KB = 1024
K_SCALES_AT = 0
V_SCALES_AT = 4 * KB
Q_RAW_AT = (6 * KB, 8 * KB)
Q_BF_AT = (10 * KB, 11 * KB)
PAIRS_AT = (12 * KB, 14 * KB, Q_RAW_AT[1])
WORDS_AT = (15 * KB, Q_RAW_AT[0], Q_RAW_AT[1] + KB, 16 * KB)
V_CODES_AT = WORDS_AT[3]
MAX_AT = (PAIRS_AT[0] + 64, PAIRS_AT[0] + 128, PAIRS_AT[0])
COLS_AT = V_CODES_AT + 4 * PAGES * DV
VS_AT = COLS_AT + 64 * PAGES


def tile_attend_pkv4_soft_kernel(tc, qT, k_words, k_scales, v_words, v_scales, vs, offs, voffs, out):
    nc = tc.nc
    with ExitStack() as ctx:
        lists = ctx.enter_context(tc.tile_pool(name="lists", bufs=1))
        sb = ctx.enter_context(tc.tile_pool(name="sb", bufs=1))
        shared = ctx.enter_context(tc.tile_pool(name="shared", bufs=1))
        ps = ctx.enter_context(tc.psum_pool(name="ps", bufs=1))

        k_list = lists.tile([P, N // 16], U16, name="k_list")
        v_list = lists.tile([P, PAGES * DV // 16], U16, name="v_list")

        k_scale_pool = shared.tile([P, T], U8, name="k_scale_pool", align_bytes=64, offset=K_SCALES_AT)
        v_scale_pool = shared.tile([P, POOL_PAGES * DV], U8, name="v_scale_pool", align_bytes=64, offset=V_SCALES_AT)
        vs_pool = shared.tile([P, T], F32, name="vs_pool", align_bytes=64, offset=VS_AT)
        k_pool = sb.tile([P, T], I32, name="k_pool", align_bytes=64)
        q_raw = [shared.tile([P, PACK, NQ], F32, name="q_raw%d" % o, align_bytes=64, offset=Q_RAW_AT[o]) for o in range(PASSES)]
        ident = sb.tile([P, P], F32, name="ident", align_bytes=64)

        nc.vector.memset(k_scale_pool[:].bitcast(I32), 0)
        nc.vector.memset(v_scale_pool[:].bitcast(I32), 0)
        nc.vector.memset(vs_pool[:, VS_FILLED:].bitcast(I32), 0)
        nc.vector.memset(ident[:], 0.0)
        make_identity(nc, ident[:], nomemset=True)

        k_rows = k_words[0].rearrange("g t b -> g (t b)").bitcast(I32)
        nc.sync.dma_start(k_pool[:, :K_FIRST], k_rows[:, :K_FIRST])
        nc.sync.dma_start(k_list[:], offs)
        nc.sync.dma_start(v_list[:], voffs)
        nc.sync.dma_start(k_scale_pool[:].bitcast(I32)[0:P:4, :], k_scales.bitcast(I32).rearrange("o f c -> f o c"))
        nc.sync.dma_start(v_scale_pool[:].bitcast(I32)[0:P:8, :].rearrange("f (u c) -> f u c", u=POOL_PAGES),
                          v_scales.bitcast(I32).rearrange("u f c -> f u c"))
        nc.sync.dma_start(k_pool[:, K_FIRST:], k_rows[:, K_FIRST:])
        q_rows = qT[0].rearrange("(o p j) w -> o p (j w)", o=PASSES, j=PACK)
        for o in range(PASSES):
            nc.sync.dma_start(q_raw[o][:].rearrange("p j w -> p (j w)"), q_rows[o])

        vs_head = sb.tile([P, VS_WIDE], F32, name="vs_head", align_bytes=64)
        nc.scalar.dma_start(vs_head[:], vs[:, :VS_WIDE])
        nc.scalar.activation(vs_pool[:, :VS_FILLED].rearrange("p (a c) -> p a c", c=VS_WIDE),
                             vs_head[:].unsqueeze(1).to_broadcast([P, VS_FILLED // VS_WIDE, VS_WIDE]), ACT.Copy)

        q_bf = [shared.tile([P, NQ, PACK], BF16, name="q_bf%d" % o, align_bytes=64, offset=Q_BF_AT[o]) for o in range(PASSES)]

        k_scale_rows = sb.tile([P, N], U8, name="k_scale_rows", align_bytes=64)
        nc.vector.tensor_copy(k_scale_rows[:], k_scale_pool[:].indirect(k_list[:]))
        k_planes = shared.tile([P, PASSES * N], U8, name="k_planes", align_bytes=64, offset=K_SCALES_AT)
        for a in (0, 2, 1, 3):
            queue = nc.sync if a < 2 else nc.scalar
            queue.dma_start(k_planes[:].bitcast(I32)[32 * a:32 * a + 4, :].rearrange("r (o c) -> r o c", o=PASSES),
                            k_scale_rows[:].bitcast(I32)[32 * a:32 * (a + 1):4, :])
        for o in range(PASSES):
            nc.scalar.activation(q_bf[o][:].rearrange("p (c i) j -> p c j i", i=PACK),
                                 q_raw[o][:].rearrange("p j (c i) -> p c j i", i=PACK), ACT.Copy, scale=-1.0)
        nc.sync.dma_start(vs_pool[VS_ROW:VS_ROW + 1, :], vs[0:1, :])
        v_pool = sb.tile([P, POOL_PAGES * DV], I32, name="v_pool", align_bytes=64)
        nc.sync.dma_start(v_pool[:].rearrange("g (u e) -> g u e", u=POOL_PAGES),
                          v_words.rearrange("u g e r -> g u (e r)").bitcast(I32))
        v_scale_rows = sb.tile([P, PAGES * DV], U8, name="v_scale_rows", align_bytes=64)
        nc.vector.tensor_copy(v_scale_rows[:], v_scale_pool[:].indirect(v_list[:]))
        v_plane = shared.tile([P, PAGES * DV], U8, name="v_plane", align_bytes=64, offset=V_SCALES_AT)
        for a in range(QUADS):
            nc.sync.dma_start(v_plane[:].bitcast(I32)[32 * a:32 * a + 4, :],
                              v_scale_rows[:].bitcast(I32)[32 * a:32 * (a + 1):8, :])

        vs_cols = []
        for g in range(PAGES):
            vs_row = sb.tile([P, PAGE], F32, name="vs_row%d" % g, align_bytes=64)
            nc.scalar.activation(vs_row[:], vs_pool[:].indirect(k_list[:, g * PAGE // 16:(g + 1) * PAGE // 16]), ACT.Copy)
            cols = shared.tile([P, PACK], F32, name="vs_cols%d" % g, align_bytes=64, offset=COLS_AT + 64 * g)
            nc.scalar.dma_start(cols[:], vs_row[VS_ROW:VS_ROW + 1, :].rearrange("o (s t) -> o s t", t=PACK))
            vs_cols.append(cols)

        chunks = ((0, PAGE), (PAGE, HALF), (PAGE + HALF, HALF))
        pairs = [None] * len(chunks)
        scores = [ps.tile([P, width], F32, name="score%d" % c) for c, (first, width) in enumerate(chunks)]
        q_codes = [sb.tile([P, NQ], U32, name="q_codes%d" % o, align_bytes=64) for o in range(PASSES)]
        q_scale = [sb.tile([P, NQ], U8, name="q_scale%d" % o, align_bytes=64) for o in range(PASSES)]

        def gather_keys(c):
            first, width = chunks[c]
            both = shared.tile([P, width], U32, name="k_pairs%d" % c, align_bytes=64, offset=PAIRS_AT[c])
            nc.vector.tensor_copy(both[:], k_pool[:].bitcast(U32).indirect(k_list[:, first // 16:(first + width) // 16]))
            pairs[c] = both[:].bitcast(U16).rearrange("p (n o) -> p o n", o=PASSES)

        def score_pass(c, o, words):
            first, width = chunks[c]
            nc.tensor.matmul_mx(
                out=scores[c][:], lhsT=q_codes[o][:].bitcast(FP8X4), lhsT_scale=q_scale[o][:],
                rhs=words.bitcast(FP4X4),
                rhs_scale=k_planes[:, o * N + first:o * N + first + width],
                start=(o == 0), stop=(o == PASSES - 1))

        gather_keys(0)
        gather_keys(1)
        for o in range(PASSES):
            words = shared.tile([P, PAGE], U16, name="k_words0_%d" % o, align_bytes=64, offset=WORDS_AT[o])
            nc.vector.tensor_copy(words[:], pairs[0][:, o, :])
            nc.vector.quantize_mx(out=q_codes[o][:].bitcast(FP8X4), scales=q_scale[o][:],
                                  in_=q_bf[o][:].rearrange("p w j -> p (w j)"))
            score_pass(0, o, words[:])
        for o in range(PASSES):
            words = shared.tile([P, HALF], U16, name="k_words1_%d" % o, align_bytes=64, offset=WORDS_AT[2] + 2 * HALF * o)
            nc.vector.tensor_copy(words[:], pairs[1][:, o, :])
            score_pass(1, o, words[:])
            if o == 0:
                gather_keys(2)
        for o in range(PASSES):
            words = shared.tile([P, HALF], U16, name="k_words2_%d" % o, align_bytes=64, offset=WORDS_AT[3] + 2 * HALF * o)
            nc.vector.tensor_copy(words[:], pairs[2][:, o, :])
            score_pass(2, o, words[:])

        neg = [sb.tile([P, PACK, width // PACK], F32, name="neg_scores%d" % c, align_bytes=64) for c, (first, width) in enumerate(chunks)]
        least = [shared.tile([P, 1], F32, name="least%d" % c, align_bytes=64, offset=MAX_AT[c]) for c in range(len(chunks))]
        for c in range(2):
            nc.vector.tensor_scalar(neg[c][:], scores[c][:].rearrange("q (s t) -> q t s", t=PACK), 1.0, None,
                                    op0=ALU.mult, op1=ALU.min, accum_out=least[c][:])
        nc.vector.tensor_scalar(neg[2][:].rearrange("q t s -> q (t s)"), scores[2][:], least[0][:], least[1][:],
                                op0=ALU.min, op1=ALU.min, accum_out=least[2][:])
        neg_max = least[2]

        v_codes = shared.tile([P, PAGES * DV], U32, name="v_codes", align_bytes=64, offset=V_CODES_AT)
        nc.vector.tensor_copy(v_codes[:], v_pool[:].bitcast(U32).indirect(v_list[:]))

        prob = shared.tile([P, N], F32, name="prob", align_bytes=64, offset=VS_AT)
        dealt = prob[:].rearrange("q (g t s) -> q g t s", g=PAGES, t=PACK)
        for t in range(PACK):
            nc.scalar.activation(dealt[:, 0, t, :], neg[0][:, t, :], ACT.Exp, bias=neg_max[:], scale=-1.0)
        last = scores[2][:].rearrange("q (s t) -> q t s", t=PACK)
        for t in range(0, PACK, 2):
            nc.scalar.activation(dealt[:, 1, t:t + 2, :P // 2], neg[1][:, t:t + 2, :], ACT.Exp, bias=neg_max[:], scale=-1.0)
            nc.scalar.activation(dealt[:, 1, t:t + 2, P // 2:], last[:, t:t + 2, :], ACT.Exp, bias=neg_max[:], scale=-1.0)
        prob_again = sb.tile([P, N], F32, name="prob_again", align_bytes=64)
        total = sb.tile([P, 1], F32, name="total")
        nc.scalar.activation(prob_again[:], prob[:], ACT.Copy, accum_out=total[:])

        y = [ps.tile([P, DV // 2], F32, name="y%d" % h) for h in range(2)]
        w_bf = []
        for g in range(PAGES):
            turned = ps.tile([P, PACK, NQ], F32, name="p_turned%d" % g)
            for t in range(PACK):
                c0 = g * PAGE + t * P
                nc.tensor.transpose(turned[:, t, :], prob[:, c0:c0 + P], ident[:])
            w = sb.tile([P, NQ, PACK], BF16, name="w_bf%d" % g, align_bytes=64)
            nc.vector.tensor_tensor(w[:], turned[:].rearrange("s t q -> s q t"),
                                    vs_cols[g][:].unsqueeze(1).to_broadcast([P, NQ, PACK]), ALU.mult)
            w_bf.append(w)
        for g in range(PAGES):
            w_codes = sb.tile([P, NQ], U32, name="w_codes%d" % g, align_bytes=64)
            w_scale = sb.tile([P, NQ], U8, name="w_scale%d" % g, align_bytes=64)
            nc.vector.quantize_mx(out=w_codes[:].bitcast(FP8X4), scales=w_scale[:],
                                  in_=w_bf[g][:].rearrange("s q t -> s (q t)"))
            for h in range(2):
                cols = slice(g * DV + h * P, g * DV + (h + 1) * P)
                nc.tensor.matmul_mx(
                    out=y[h][:], lhsT=w_codes[:].bitcast(FP8X4), lhsT_scale=w_scale[:],
                    rhs=v_codes[:, cols].bitcast(FP8X4), rhs_scale=v_plane[:, cols],
                    start=(g == 0), stop=(g == PAGES - 1))

        inv = shared.tile([P, 1], F32, name="inv", align_bytes=64, offset=COLS_AT + 64 * (PAGES - 1))
        nc.vector.reciprocal(inv[:], total[:])
        res = [sb.tile([P, DV // 2], F32, name="res%d" % h, align_bytes=64) for h in range(2)]
        nc.vector.tensor_scalar(res[0][:], y[0][:], inv[:], None, op0=ALU.mult)
        nc.sync.dma_start(out[0][:, :P], res[0][:])
        nc.scalar.activation(res[1][:], y[1][:], ACT.Copy, scale=inv[:])
        nc.scalar.dma_start(out[0][:, P:], res[1][:])
